import numpy as np
import ml_dtypes


def mxq(x, axis, fmt="e4m3"):
    dtype, down = {"e4m3": (ml_dtypes.float8_e4m3fn, 7), "e5m2": (ml_dtypes.float8_e5m2, 14)}[fmt]
    v = np.moveaxis(np.asarray(x, np.float32).astype(ml_dtypes.bfloat16).astype(np.float64), axis, -1)
    blocks = v.reshape(v.shape[:-1] + (-1, 32))
    amax = np.abs(blocks).max(-1, keepdims=True)
    byte = np.maximum(np.where(amax > 0, np.frexp(amax)[1] - 1 + 127, 0) - down, 1)
    scale = np.exp2(byte - 127.0)
    codes = (blocks / scale).astype(np.float32).astype(dtype).astype(np.float64)
    return np.moveaxis((codes * scale).reshape(v.shape), -1, axis)


WIDE = False


def mx_kscale(k):
    if not WIDE:
        return np.ones(k)
    levels = np.array([10, -10, 5, -5, 0])
    if k % 512:
        return np.exp2(np.random.permutation(np.resize(levels, k // 32))).repeat(32)
    a = np.empty((k // 512, 16))
    for p in range(k // 512):
        a[p, :8] = np.random.permutation(np.resize(levels, 8))
        for g in range(8):
            far = levels[np.abs(levels - a[p, g]) >= 10]
            a[p, g + 8] = far[np.random.randint(len(far))]
    return np.exp2(a.ravel()).repeat(32)


def f64(x):
    return np.asarray(x).astype(np.float64)


def striped(idx):
    return np.tile(idx.reshape(-1, 16).T, (8, 1)).astype(np.uint16)


def unstriped(offs):
    return offs[:16].T.reshape(-1).astype(np.int64)


E2M1 = np.array([0.0, 0.5, 1.0, 1.5, 2.0, 3.0, 4.0, 6.0, -0.0, -0.5, -1.0, -1.5, -2.0, -3.0, -4.0, -6.0])


def pack_weight(w, fmt):
    k, n = w.shape
    w = f64(np.asarray(w, np.float32).astype(ml_dtypes.bfloat16)).reshape(k // 32, 32, n)
    amax = np.abs(w).max(1)
    if fmt == "e4m3":
        byte = np.frexp(amax)[1] - 1 + 127 - 7
    else:
        mant, ex = np.frexp(amax / 6.0)
        byte = np.where(mant > 0.5, ex, ex - 1) + 127
    byte = np.clip(np.where(amax > 0, byte, 1), 1, 254)
    scaled = (w * np.exp2(127.0 - byte)[:, None, :]).reshape(k, n).astype(np.float32)
    by_word = np.ascontiguousarray(scaled.reshape(k // 512, 128, 4, n).transpose(0, 1, 3, 2))
    if fmt == "e4m3":
        words = by_word.astype(ml_dtypes.float8_e4m3fn).view(np.uint8)
    else:
        c = by_word.astype(ml_dtypes.float4_e2m1fn).view(np.uint8) & 0xF
        words = (c[..., 0::2] | (c[..., 1::2] << 4)).reshape(k // 512, 128, 2 * n)
    return np.ascontiguousarray(words), np.ascontiguousarray(byte.astype(np.uint8).reshape(k // 512, 16, n))


def unpack_weight(words, scales, fmt):
    g, _, n = scales.shape
    words = np.ascontiguousarray(words).reshape(g, 128, n, -1)
    if fmt == "e4m3":
        vals = words.view(ml_dtypes.float8_e4m3fn).astype(np.float64)
    else:
        nib = np.empty((g, 128, n, 4), np.uint8)
        nib[..., 0::2] = words & 0xF
        nib[..., 1::2] = words >> 4
        vals = E2M1[nib]
    vals = vals * np.repeat(np.exp2(scales.astype(np.float64) - 127.0), 8, axis=1)[..., None]
    return vals.transpose(0, 1, 3, 2).reshape(g * 512, n)


def relu(v):
    return np.maximum(v, 0.0)


K, T, E, C, F, D, H = 512, 512, 2, 256, 2, 256, 512
N = 512


def by_expert(wq, xq, E, C):
    return np.concatenate([wq[e].T @ xq[:, e * C:(e + 1) * C] for e in range(E)], axis=1)


def setup_inputs():
    n = np.random.standard_normal
    s = mx_kscale(K)
    u = mx_kscale(H)
    slot_token = np.random.permutation(T)[:E * C]
    slots2 = np.random.permutation(T)[:F * D]
    x = pack_weight(n((K, T)) * s[:, None], "e4m3")
    w = [pack_weight(m, "e4m3") for m in n((E, K, N)) / np.sqrt(K) / s[None, :, None]]
    wa = [pack_weight(m, "e4m3") for m in n((F, K, H)) / np.sqrt(K) / s[None, :, None] * u]
    wb = [pack_weight(m, "e4m3") for m in n((F, H, N)) / np.sqrt(H) / u[None, :, None]]
    return {
        "x_words": x[0],
        "x_scales": x[1],
        "w_words": np.stack([m[0] for m in w]),
        "w_scales": np.stack([m[1] for m in w]),
        "wa_words": np.stack([m[0] for m in wa]),
        "wa_scales": np.stack([m[1] for m in wa]),
        "wb_words": np.stack([m[0] for m in wb]),
        "wb_scales": np.stack([m[1] for m in wb]),
        "gate": np.tile(np.random.uniform(0.2, 1.0, E * C), (128, 1)).astype(np.float32),
        "gate2": (np.tile(np.random.uniform(0.2, 1.0, F * D), (128, 1))).astype(np.float32),
        "offs": striped(slot_token),
        "offs2": striped(slots2),
    }


def reference(x_words, x_scales, w_words, w_scales, wa_words, wa_scales, wb_words, wb_scales, gate, gate2, offs, offs2):
    w = np.stack([unpack_weight(w_words[e], w_scales[e], "e4m3") for e in range(E)])
    wa = np.stack([unpack_weight(wa_words[e], wa_scales[e], "e4m3") for e in range(F)])
    wb = np.stack([unpack_weight(wb_words[e], wb_scales[e], "e4m3") for e in range(F)])
    idx, idx2 = unstriped(offs), unstriped(offs2)
    x = unpack_weight(x_words, x_scales, "e4m3")
    y = by_expert(w, x[:, idx], E, C)
    h = relu(by_expert(wa, x[:, idx2], F, D))
    z = by_expert(wb, mxq(h, 0, "e4m3"), F, D)
    out = np.zeros((N, T))
    out[:, idx] = f64(gate[:1]) * y
    out[:, idx2] += f64(gate2[:1]) * z
    return out

@@ -1,0 +1,211 @@
+from contextlib import ExitStack
+
+import concourse.mybir as mybir
+from concourse.masks import make_identity
+
+K, T, N, H = 512, 512, 512, 512
+E, C = 2, 256
+FLOPS = 2 * (K * N + K * H + H * N) * T
+
+F32 = mybir.dt.float32
+BF16 = mybir.dt.bfloat16
+I32 = mybir.dt.int32
+U32 = mybir.dt.uint32
+U16 = mybir.dt.uint16
+U8 = mybir.dt.uint8
+FP8X4 = mybir.dt.float8_e4m3fn_x4
+RELU = mybir.ActivationFunctionType.Relu
+MULT = mybir.AluOpType.mult
+ADD = mybir.AluOpType.add
+
+P = 128
+PACK = 4
+TILES = N // P
+LIST = 16
+WINDOW = 768
+
+
+def tile_moe_mlr_relu_kernel(
+    tc, x_words, x_scales, w_words, w_scales, wa_words, wa_scales, wb_words, wb_scales, gate, gate2, offs, offs2, out
+):
+    nc = tc.nc
+    with ExitStack() as ctx:
+        keep = ctx.enter_context(tc.tile_pool(name="keep", bufs=1))
+        stage = ctx.enter_context(tc.tile_pool(name="stage", bufs=2))
+        psum = ctx.enter_context(tc.psum_pool(name="psum", bufs=1))
+
+        def plane_tile(name, count):
+            tile = keep.tile([P, count, T], U8, name=name, align_bytes=64)
+            nc.vector.memset(tile[:].bitcast(I32), 0)
+            return tile
+
+        def load_planes(queue, tile, scales):
+            rows = scales.bitcast(I32)
+            for q in range(4):
+                queue.dma_start(
+                    out=tile[32 * q : 32 * q + 4, :, :].bitcast(I32),
+                    in_=rows[:, 4 * q : 4 * q + 4, :].rearrange("e r n -> r e n"),
+                )
+
+        def load_words(name, words):
+            count = words.shape[0]
+            tile = keep.tile([P, count, T], I32, name=name, align_bytes=64)
+            nc.sync.dma_start(out=tile[:], in_=words.rearrange("e p n d -> p e (n d)").bitcast(I32))
+            return tile
+
+        def load_list(name, source):
+            tile = keep.tile([P, T // LIST], U16, name=name)
+            nc.sync.dma_start(tile[:], source)
+            return tile
+
+        def load_gate(name, source):
+            tile = keep.tile([P, T], F32, name=name)
+            nc.sync.dma_start(out=tile[:], in_=source)
+            return tile
+
+        x_plane = plane_tile("x_plane", 1)
+        w_plane = plane_tile("w_plane", E)
+        wa_plane = plane_tile("wa_plane", E)
+        wb_plane = plane_tile("wb_plane", E)
+
+        expert_list = load_list("expert_list", offs)
+        x_sb = load_words("x_sb", x_words)
+        load_planes(nc.scalar, x_plane, x_scales)
+        adapter_list = load_list("adapter_list", offs2)
+        w_sb = load_words("w_sb", w_words[:, 0])
+        load_planes(nc.sync, w_plane, w_scales[:, 0])
+        gate_sb = load_gate("gate_sb", gate)
+        wa_sb = load_words("wa_sb", wa_words[:, 0])
+        wb_sb = load_words("wb_sb", wb_words[:, 0])
+        load_planes(nc.sync, wb_plane, wb_scales[:, 0])
+        gate2_sb = load_gate("gate2_sb", gate2)
+
+        ident_f32 = keep.tile([P, P], F32, name="ident_f32")
+        make_identity(nc, ident_f32[:])
+        ident_bf16 = keep.tile([P, P], BF16, name="ident_bf16")
+        nc.scalar.activation(ident_bf16[:], ident_f32[:], RELU)
+        load_planes(nc.gpsimd, wa_plane, wa_scales[:, 0])
+
+        def gather_tokens(name, slots):
+            words = keep.tile([P, T], U32, name=name + "_words", align_bytes=64)
+            plane = keep.tile([P, T], U8, name=name + "_plane", align_bytes=64)
+            for e in range(E):
+                cols = slice(e * C, (e + 1) * C)
+                entries = slots[:, e * C // LIST : (e + 1) * C // LIST]
+                nc.vector.tensor_copy(words[:, cols], x_sb[:, 0, :].bitcast(U32).indirect(entries))
+                nc.vector.tensor_copy(plane[:, cols], x_plane[:, 0, :].indirect(entries))
+            return words, plane
+
+        def project(bank, tag, j, weights, weight_plane, words, plane):
+            acc = psum.tile([P, T], F32, name=bank)
+            rows = slice(j * P, (j + 1) * P)
+            for e in range(E):
+                cols = slice(e * C, (e + 1) * C)
+                nc.tensor.matmul_mx(
+                    out=acc[:, cols],
+                    lhsT=weights[:, e, rows].bitcast(FP8X4),
+                    lhsT_scale=weight_plane[:, e, rows],
+                    rhs=words[:, cols].bitcast(FP8X4),
+                    rhs_scale=plane[:, cols],
+                    start=True,
+                    stop=True,
+                )
+            by_slot = keep.tile([P, T], F32, name=tag, align_bytes=64)
+            nc.scalar.copy(by_slot[:], acc[:])
+            return by_slot
+
+        def scatter(tag, by_slot, weight, slots):
+            by_token = keep.tile([P, WINDOW], F32, name=tag, align_bytes=64)
+            nc.vector.tensor_tensor(by_token[:].indirect(slots[:]), by_slot[:], weight[:], MULT)
+            return by_token
+
+        def hidden_block(b, grouped, words, plane):
+            cols = slice(b * P, (b + 1) * P)
+            f = b * P // C
+            acc = psum.tile([P, H], F32, name=f"bank{(b + 2) % 4}")
+            nc.tensor.matmul_mx(
+                out=acc[:],
+                lhsT=words[:, cols].bitcast(FP8X4),
+                lhsT_scale=plane[:, cols],
+                rhs=wa_sb[:, f, :].bitcast(FP8X4),
+                rhs_scale=wa_plane[:, f, :],
+                start=True,
+                stop=True,
+            )
+            h_rows = keep.tile([P, PACK, P], BF16, name=f"h_rows{b}", align_bytes=64)
+            nc.scalar.activation(h_rows[:], acc[:].rearrange("m (p d) -> m d p", d=PACK), RELU)
+            return h_rows
+
+        def turn_block(b, grouped, h_rows):
+            turned = psum.tile([P, PACK, P], BF16, name="turned", bufs=2)
+            for d in range(PACK):
+                nc.tensor.transpose(turned[:, d, :], h_rows[:, d, :], ident_bf16[:])
+            nc.scalar.copy(grouped[:, b * P : (b + 1) * P, :], turned[:].rearrange("p d m -> p m d"))
+
+        def turn_into_sum(sum_t, by_token, first):
+            blocks = T // P
+            for b in range(blocks):
+                cols = slice(b * P, (b + 1) * P)
+                nc.tensor.matmul(
+                    sum_t[:, cols],
+                    by_token[:, cols],
+                    ident_f32[:],
+                    start=first and b == 0,
+                    stop=not first and b == blocks - 1,
+                    is_transpose=True,
+                )
+
+        def open_sum(j, o_tokens):
+            sum_t = psum.tile([P, T], F32, name=f"bank{(j + 2) % 4}")
+            turn_into_sum(sum_t, o_tokens, True)
+            return sum_t
+
+        def close_sum(j, sum_t, z_tokens):
+            turn_into_sum(sum_t, z_tokens, False)
+            sum_t_sb = stage.tile([P, T], F32, name="sum_t_sb")
+            nc.scalar.copy(sum_t_sb[:], sum_t[:])
+            back = psum.tile([P, T], F32, name="turned", bufs=2)
+            for b in range(T // P):
+                cols = slice(b * P, (b + 1) * P)
+                nc.tensor.transpose(back[:, cols], sum_t_sb[:, cols], ident_f32[:])
+            result = stage.tile([P, T], F32, name="result")
+            nc.scalar.copy(result[:], back[:])
+            nc.scalar.dma_start(out=out[j * P : (j + 1) * P, :], in_=result[:])
+
+        xe_words, xe_plane = gather_tokens("xe", expert_list)
+        xa_words, xa_plane = gather_tokens("xa", adapter_list)
+
+        def expert_tile(j, bank, tag):
+            return project(bank, tag, j, w_sb, w_plane, xe_words, xe_plane)
+
+        def adapter_tile(j):
+            return project(f"bank{(j + 2) % 4}", f"z_slots{j}", j, wb_sb, wb_plane, h_words, h_plane)
+
+        y = [expert_tile(j, f"bank{j}", f"y_slots{j}") for j in range(2)]
+        o = [scatter(f"y_tokens{j}", y[j], gate_sb, expert_list) for j in range(2)]
+
+        grouped = keep.tile([P, T, PACK], BF16, name="grouped", align_bytes=64)
+        h_blocks = [hidden_block(b, grouped, xa_words, xa_plane) for b in range(T // P)]
+        for b in range(T // P):
+            turn_block(b, grouped, h_blocks[b])
+        h_words = keep.tile([P, T], U32, name="h_words", align_bytes=64)
+        h_plane = keep.tile([P, T], U8, name="h_plane", align_bytes=64)
+        nc.vector.quantize_mx(
+            out=h_words[:].bitcast(FP8X4), scales=h_plane[:], in_=grouped[:].rearrange("p m d -> p (m d)")
+        )
+
+        last = TILES - 1
+        o.append(scatter("y_tokens2", expert_tile(2, "bank4", "h_rows3"), gate_sb, expert_list))
+        z = [adapter_tile(j) for j in range(TILES)]
+        y_last = expert_tile(last, "bank5", "grouped")
+        sums = [open_sum(j, o[j]) for j in range(last)]
+        for j in range(last):
+            close_sum(j, sums[j], scatter(f"z_tokens{j}", z[j], gate2_sb, adapter_list))
+
+        o_last = scatter("z_slots1", y_last, gate_sb, expert_list)
+        z_last = scatter("z_tokens3", z[last], gate2_sb, adapter_list)
+        final = keep.tile([P, T], F32, name="final")
+        half = T // 2
+        for cols in (slice(0, half), slice(half, T)):
+            nc.vector.tensor_tensor(final[:, cols], o_last[:, cols], z_last[:, cols], ADD)
+            nc.sync.dma_start(out=out[last * P :, cols], in_=final[:, cols])

@@ -71,11 +71,15 @@ def tile_moe_mlr_relu_kernel(
         expert_list = load_list("expert_list", offs)
         x_sb = load_words("x_sb", x_words)
         load_planes(nc.scalar, x_plane, x_scales)
-        adapter_list = load_list("adapter_list", offs2)
-        w_sb = load_words("w_sb", w_words[:, 0])
         load_planes(nc.sync, w_plane, w_scales[:, 0])
+        w_sb = keep.tile([P, E, T], I32, name="w_sb", align_bytes=64)
+        w_rows = w_words[:, 0].rearrange("e p n d -> p e (n d)").bitcast(I32)
+        nc.sync.dma_start(out=w_sb[:, 0, :], in_=w_rows[:, 0, :])
+        adapter_list = load_list("adapter_list", offs2)
+        nc.sync.dma_start(out=w_sb[:, 1, :], in_=w_rows[:, 1, :])
         gate_sb = load_gate("gate_sb", gate)
         wa_sb = load_words("wa_sb", wa_words[:, 0])
+        load_planes(nc.sync, wa_plane, wa_scales[:, 0])
         wb_sb = load_words("wb_sb", wb_words[:, 0])
         load_planes(nc.sync, wb_plane, wb_scales[:, 0])
         gate2_sb = load_gate("gate2_sb", gate2)
@@ -84,7 +88,6 @@ def tile_moe_mlr_relu_kernel(
         make_identity(nc, ident_f32[:])
         ident_bf16 = keep.tile([P, P], BF16, name="ident_bf16")
         nc.scalar.activation(ident_bf16[:], ident_f32[:], RELU)
-        load_planes(nc.gpsimd, wa_plane, wa_scales[:, 0])
 
         def gather_tokens(name, slots):
             words = keep.tile([P, T], U32, name=name + "_words", align_bytes=64)
@@ -181,8 +184,25 @@ def tile_moe_mlr_relu_kernel(
         def adapter_tile(j):
             return project(f"bank{(j + 2) % 4}", f"z_slots{j}", j, wb_sb, wb_plane, h_words, h_plane)
 
-        y = [expert_tile(j, f"bank{j}", f"y_slots{j}") for j in range(2)]
-        o = [scatter(f"y_tokens{j}", y[j], gate_sb, expert_list) for j in range(2)]
+        o = [keep.tile([P, T], F32, name=f"y_tokens{j}") for j in range(2)]
+        for e in range(E):
+            cols = slice(e * C, (e + 1) * C)
+            for j in range(2):
+                rows = slice(j * P, (j + 1) * P)
+                acc = psum.tile([P, C], F32, name=f"bank{(0, 1, 4, 5)[2 * e + j]}")
+                nc.tensor.matmul_mx(
+                    out=acc[:],
+                    lhsT=w_sb[:, e, rows].bitcast(FP8X4),
+                    lhsT_scale=w_plane[:, e, rows],
+                    rhs=xe_words[:, cols].bitcast(FP8X4),
+                    rhs_scale=xe_plane[:, cols],
+                    start=True,
+                    stop=True,
+                )
+                by_slot = keep.tile([P, C], F32, name=f"y_half{e}{j}")
+                nc.scalar.copy(by_slot[:], acc[:])
+                entries = expert_list[:, e * C // LIST : (e + 1) * C // LIST]
+                nc.vector.tensor_tensor(o[j][:].indirect(entries), by_slot[:], gate_sb[:, cols], MULT)
 
         grouped = keep.tile([P, T, PACK], BF16, name="grouped", align_bytes=64)
         h_blocks = [hidden_block(b, grouped, xa_words, xa_plane) for b in range(T // P)]

@@ -34,18 +34,12 @@ def tile_moe_mlr_relu_kernel(
         stage = ctx.enter_context(tc.tile_pool(name="stage", bufs=2))
         psum = ctx.enter_context(tc.psum_pool(name="psum", bufs=1))
 
-        def plane_tile(name, count):
-            tile = keep.tile([P, count, T], U8, name=name, align_bytes=64)
-            nc.vector.memset(tile[:].bitcast(I32), 0)
-            return tile
-
-        def load_planes(queue, tile, scales):
+        def load_planes(queue, tile, first_row, scales):
+            count = scales.shape[0]
             rows = scales.bitcast(I32)
             for q in range(4):
-                queue.dma_start(
-                    out=tile[32 * q : 32 * q + 4, :, :].bitcast(I32),
-                    in_=rows[:, 4 * q : 4 * q + 4, :].rearrange("e r n -> r e n"),
-                )
+                start = 32 * q + first_row
+                queue.dma_start(out=tile[start : start + 4 * count, :].bitcast(I32), in_=rows[:, 4 * q : 4 * q + 4, :])
 
         def load_words(name, words):
             count = words.shape[0]
@@ -63,25 +57,25 @@ def tile_moe_mlr_relu_kernel(
             nc.sync.dma_start(out=tile[:], in_=source)
             return tile
 
-        x_plane = plane_tile("x_plane", 1)
-        w_plane = plane_tile("w_plane", E)
-        wa_plane = plane_tile("wa_plane", E)
-        wb_plane = plane_tile("wb_plane", E)
+        x_plane = keep.tile([P, T], U8, name="x_plane", align_bytes=64)
+        nc.vector.memset(x_plane[:].bitcast(I32), 0)
+        planes = {}
+        for name in ("w", "wa", "wb"):
+            planes[name] = keep.tile([P, T], U8, name=name + "_plane", align_bytes=64)
+            nc.vector.memset(planes[name][:].bitcast(I32), 0)
+        w_plane, wa_plane, wb_plane = planes["w"], planes["wa"], planes["wb"]
 
         expert_list = load_list("expert_list", offs)
         x_sb = load_words("x_sb", x_words)
-        load_planes(nc.scalar, x_plane, x_scales)
-        load_planes(nc.sync, w_plane, w_scales[:, 0])
-        w_sb = keep.tile([P, E, T], I32, name="w_sb", align_bytes=64)
-        w_rows = w_words[:, 0].rearrange("e p n d -> p e (n d)").bitcast(I32)
-        nc.sync.dma_start(out=w_sb[:, 0, :], in_=w_rows[:, 0, :])
+        load_planes(nc.sync, x_plane, 0, x_scales)
         adapter_list = load_list("adapter_list", offs2)
-        nc.sync.dma_start(out=w_sb[:, 1, :], in_=w_rows[:, 1, :])
+        w_sb = load_words("w_sb", w_words[:, 0])
+        load_planes(nc.sync, w_plane, 0, w_scales[:, 0])
         gate_sb = load_gate("gate_sb", gate)
         wa_sb = load_words("wa_sb", wa_words[:, 0])
-        load_planes(nc.sync, wa_plane, wa_scales[:, 0])
+        load_planes(nc.sync, wa_plane, 8, wa_scales[:, 0])
+        load_planes(nc.sync, wb_plane, 0, wb_scales[:, 0])
         wb_sb = load_words("wb_sb", wb_words[:, 0])
-        load_planes(nc.sync, wb_plane, wb_scales[:, 0])
         gate2_sb = load_gate("gate2_sb", gate2)
 
         ident_f32 = keep.tile([P, P], F32, name="ident_f32")
@@ -96,7 +90,10 @@ def tile_moe_mlr_relu_kernel(
                 cols = slice(e * C, (e + 1) * C)
                 entries = slots[:, e * C // LIST : (e + 1) * C // LIST]
                 nc.vector.tensor_copy(words[:, cols], x_sb[:, 0, :].bitcast(U32).indirect(entries))
-                nc.vector.tensor_copy(plane[:, cols], x_plane[:, 0, :].indirect(entries))
+            for e in range(E):
+                cols = slice(e * C, (e + 1) * C)
+                entries = slots[:, e * C // LIST : (e + 1) * C // LIST]
+                nc.vector.tensor_copy(plane[:, cols], x_plane[:].indirect(entries))
             return words, plane
 
         def project(bank, tag, j, weights, weight_plane, words, plane):
@@ -107,7 +104,7 @@ def tile_moe_mlr_relu_kernel(
                 nc.tensor.matmul_mx(
                     out=acc[:, cols],
                     lhsT=weights[:, e, rows].bitcast(FP8X4),
-                    lhsT_scale=weight_plane[:, e, rows],
+                    lhsT_scale=weight_plane[4 * e :, rows],
                     rhs=words[:, cols].bitcast(FP8X4),
                     rhs_scale=plane[:, cols],
                     start=True,
@@ -131,7 +128,7 @@ def tile_moe_mlr_relu_kernel(
                 lhsT=words[:, cols].bitcast(FP8X4),
                 lhsT_scale=plane[:, cols],
                 rhs=wa_sb[:, f, :].bitcast(FP8X4),
-                rhs_scale=wa_plane[:, f, :],
+                rhs_scale=wa_plane[8 + 4 * f :, :],
                 start=True,
                 stop=True,
             )
@@ -193,7 +190,7 @@ def tile_moe_mlr_relu_kernel(
                 nc.tensor.matmul_mx(
                     out=acc[:],
                     lhsT=w_sb[:, e, rows].bitcast(FP8X4),
-                    lhsT_scale=w_plane[:, e, rows],
+                    lhsT_scale=w_plane[4 * e :, rows],
                     rhs=xe_words[:, cols].bitcast(FP8X4),
                     rhs_scale=xe_plane[:, cols],
                     start=True,

@@ -39,7 +39,7 @@ def tile_moe_mlr_relu_kernel(
             rows = scales.bitcast(I32)
             for q in range(4):
                 start = 32 * q + first_row
-                queue.dma_start(out=tile[start : start + 4 * count, :].bitcast(I32), in_=rows[:, 4 * q : 4 * q + 4, :])
+                queue.dma_start(out=tile[start : start + 4 * count, :T].bitcast(I32), in_=rows[:, 4 * q : 4 * q + 4, :])
 
         def load_words(name, words):
             count = words.shape[0]
@@ -57,7 +57,7 @@ def tile_moe_mlr_relu_kernel(
             nc.sync.dma_start(out=tile[:], in_=source)
             return tile
 
-        x_plane = keep.tile([P, T], U8, name="x_plane", align_bytes=64)
+        x_plane = keep.tile([P, WINDOW], U8, name="x_plane", align_bytes=64)
         nc.vector.memset(x_plane[:].bitcast(I32), 0)
         planes = {}
         for name in ("w", "wa", "wb"):
@@ -66,7 +66,8 @@ def tile_moe_mlr_relu_kernel(
         w_plane, wa_plane, wb_plane = planes["w"], planes["wa"], planes["wb"]
 
         expert_list = load_list("expert_list", offs)
-        x_sb = load_words("x_sb", x_words)
+        x_sb = keep.tile([P, WINDOW], I32, name="x_sb", align_bytes=64)
+        nc.sync.dma_start(out=x_sb[:, :T], in_=x_words[0].rearrange("p t d -> p (t d)").bitcast(I32))
         load_planes(nc.sync, x_plane, 0, x_scales)
         adapter_list = load_list("adapter_list", offs2)
         w_sb = load_words("w_sb", w_words[:, 0])
@@ -86,14 +87,8 @@ def tile_moe_mlr_relu_kernel(
         def gather_tokens(name, slots):
             words = keep.tile([P, T], U32, name=name + "_words", align_bytes=64)
             plane = keep.tile([P, T], U8, name=name + "_plane", align_bytes=64)
-            for e in range(E):
-                cols = slice(e * C, (e + 1) * C)
-                entries = slots[:, e * C // LIST : (e + 1) * C // LIST]
-                nc.vector.tensor_copy(words[:, cols], x_sb[:, 0, :].bitcast(U32).indirect(entries))
-            for e in range(E):
-                cols = slice(e * C, (e + 1) * C)
-                entries = slots[:, e * C // LIST : (e + 1) * C // LIST]
-                nc.vector.tensor_copy(plane[:, cols], x_plane[:].indirect(entries))
+            nc.vector.tensor_copy(words[:], x_sb[:].bitcast(U32).indirect(slots[:]))
+            nc.vector.tensor_copy(plane[:], x_plane[:].indirect(slots[:]))
             return words, plane
 
         def project(bank, tag, j, weights, weight_plane, words, plane):
@@ -181,25 +176,7 @@ def tile_moe_mlr_relu_kernel(
         def adapter_tile(j):
             return project(f"bank{(j + 2) % 4}", f"z_slots{j}", j, wb_sb, wb_plane, h_words, h_plane)
 
-        o = [keep.tile([P, T], F32, name=f"y_tokens{j}") for j in range(2)]
-        for e in range(E):
-            cols = slice(e * C, (e + 1) * C)
-            for j in range(2):
-                rows = slice(j * P, (j + 1) * P)
-                acc = psum.tile([P, C], F32, name=f"bank{(0, 1, 4, 5)[2 * e + j]}")
-                nc.tensor.matmul_mx(
-                    out=acc[:],
-                    lhsT=w_sb[:, e, rows].bitcast(FP8X4),
-                    lhsT_scale=w_plane[4 * e :, rows],
-                    rhs=xe_words[:, cols].bitcast(FP8X4),
-                    rhs_scale=xe_plane[:, cols],
-                    start=True,
-                    stop=True,
-                )
-                by_slot = keep.tile([P, C], F32, name=f"y_half{e}{j}")
-                nc.scalar.copy(by_slot[:], acc[:])
-                entries = expert_list[:, e * C // LIST : (e + 1) * C // LIST]
-                nc.vector.tensor_tensor(o[j][:].indirect(entries), by_slot[:], gate_sb[:, cols], MULT)
+        o = [scatter(f"y_tokens{j}", expert_tile(j, f"bank{j}", f"y_slots{j}"), gate_sb, expert_list) for j in range(2)]
 
         grouped = keep.tile([P, T, PACK], BF16, name="grouped", align_bytes=64)
         h_blocks = [hidden_block(b, grouped, xa_words, xa_plane) for b in range(T // P)]

@@ -58,7 +58,6 @@ def tile_moe_mlr_relu_kernel(
             return tile
 
         x_plane = keep.tile([P, WINDOW], U8, name="x_plane", align_bytes=64)
-        nc.vector.memset(x_plane[:].bitcast(I32), 0)
         planes = {}
         for name in ("w", "wa", "wb"):
             planes[name] = keep.tile([P, T], U8, name=name + "_plane", align_bytes=64)
@@ -66,9 +65,14 @@ def tile_moe_mlr_relu_kernel(
         w_plane, wa_plane, wb_plane = planes["w"], planes["wa"], planes["wb"]
 
         expert_list = load_list("expert_list", offs)
+        x_rows = x_scales.bitcast(I32)
+        for q, queue in enumerate((nc.scalar, nc.scalar, nc.sync, nc.sync)):
+            queue.dma_start(
+                out=x_plane[32 * q : 32 * (q + 1), :T].bitcast(I32),
+                in_=x_rows[:, 4 * q : 4 * q + 4, :].broadcast_to([8, 4, T // 4]),
+            )
         x_sb = keep.tile([P, WINDOW], I32, name="x_sb", align_bytes=64)
         nc.sync.dma_start(out=x_sb[:, :T], in_=x_words[0].rearrange("p t d -> p (t d)").bitcast(I32))
-        load_planes(nc.sync, x_plane, 0, x_scales)
         adapter_list = load_list("adapter_list", offs2)
         w_sb = load_words("w_sb", w_words[:, 0])
         load_planes(nc.sync, w_plane, 0, w_scales[:, 0])
@@ -87,8 +91,8 @@ def tile_moe_mlr_relu_kernel(
         def gather_tokens(name, slots):
             words = keep.tile([P, T], U32, name=name + "_words", align_bytes=64)
             plane = keep.tile([P, T], U8, name=name + "_plane", align_bytes=64)
-            nc.vector.tensor_copy(words[:], x_sb[:].bitcast(U32).indirect(slots[:]))
             nc.vector.tensor_copy(plane[:], x_plane[:].indirect(slots[:]))
+            nc.vector.tensor_copy(words[:], x_sb[:].bitcast(U32).indirect(slots[:]))
             return words, plane
 
         def project(bank, tag, j, weights, weight_plane, words, plane):

@@ -34,16 +34,16 @@ def tile_moe_mlr_relu_kernel(
         stage = ctx.enter_context(tc.tile_pool(name="stage", bufs=2))
         psum = ctx.enter_context(tc.psum_pool(name="psum", bufs=1))
 
-        def load_planes(queue, tile, first_row, scales):
+        def load_planes(queue, tile, first_row, scales, quadrants=range(4)):
             count = scales.shape[0]
             rows = scales.bitcast(I32)
-            for q in range(4):
+            for q in quadrants:
                 start = 32 * q + first_row
                 queue.dma_start(out=tile[start : start + 4 * count, :T].bitcast(I32), in_=rows[:, 4 * q : 4 * q + 4, :])
 
         def load_words(name, words):
             count = words.shape[0]
-            tile = keep.tile([P, count, T], I32, name=name, align_bytes=64)
+            tile = keep.tile([P, count, words.shape[2]], I32, name=name, align_bytes=64)
             nc.sync.dma_start(out=tile[:], in_=words.rearrange("e p n d -> p e (n d)").bitcast(I32))
             return tile
 
@@ -64,8 +64,17 @@ def tile_moe_mlr_relu_kernel(
             nc.vector.memset(planes[name][:].bitcast(I32), 0)
         w_plane, wa_plane, wb_plane = planes["w"], planes["wa"], planes["wb"]
 
-        expert_list = load_list("expert_list", offs)
+        xa_plane = keep.tile([P, T], U8, name="xa_plane", align_bytes=64)
+        nc.vector.memset(xa_plane[:].bitcast(I32), 0)
+
+        adapter_list = load_list("adapter_list", offs2)
         x_rows = x_scales.bitcast(I32)
+        x_spread = keep.tile([P, WINDOW], U8, name="x_spread", align_bytes=64)
+        nc.scalar.dma_start(
+            out=x_spread[:, :T].bitcast(I32),
+            in_=x_rows.rearrange("s b w -> b s w").broadcast_to([16, 8, T // 4]),
+        )
+        expert_list = load_list("expert_list", offs)
         for q, queue in enumerate((nc.scalar, nc.scalar, nc.sync, nc.sync)):
             queue.dma_start(
                 out=x_plane[32 * q : 32 * (q + 1), :T].bitcast(I32),
@@ -73,36 +82,47 @@ def tile_moe_mlr_relu_kernel(
             )
         x_sb = keep.tile([P, WINDOW], I32, name="x_sb", align_bytes=64)
         nc.sync.dma_start(out=x_sb[:, :T], in_=x_words[0].rearrange("p t d -> p (t d)").bitcast(I32))
-        adapter_list = load_list("adapter_list", offs2)
-        w_sb = load_words("w_sb", w_words[:, 0])
+        w_low = load_words("w_low", w_words[:, 0, :, : N // 2])
         load_planes(nc.sync, w_plane, 0, w_scales[:, 0])
+        load_planes(nc.sync, wa_plane, 8, wa_scales[:, 0], range(1))
         gate_sb = load_gate("gate_sb", gate)
         wa_sb = load_words("wa_sb", wa_words[:, 0])
-        load_planes(nc.sync, wa_plane, 8, wa_scales[:, 0])
+        load_planes(nc.sync, wa_plane, 8, wa_scales[:, 0], range(1, 4))
+        xa_spread = keep.tile([P, T], U8, name="xa_spread", align_bytes=64)
+        nc.vector.tensor_copy(xa_spread[:], x_spread[:].indirect(adapter_list[:]))
+        for q in range(4):
+            nc.sync.dma_start(
+                out=xa_plane[32 * q : 32 * q + 4, :].bitcast(I32),
+                in_=xa_spread[32 * q : 32 * (q + 1) : 8, :].bitcast(I32),
+            )
+        w_high = load_words("w_high", w_words[:, 0, :, N // 2 :])
         load_planes(nc.sync, wb_plane, 0, wb_scales[:, 0])
         wb_sb = load_words("wb_sb", wb_words[:, 0])
         gate2_sb = load_gate("gate2_sb", gate2)
 
         ident_f32 = keep.tile([P, P], F32, name="ident_f32")
         make_identity(nc, ident_f32[:])
-        ident_bf16 = keep.tile([P, P], BF16, name="ident_bf16")
-        nc.scalar.activation(ident_bf16[:], ident_f32[:], RELU)
 
         def gather_tokens(name, slots):
             words = keep.tile([P, T], U32, name=name + "_words", align_bytes=64)
             plane = keep.tile([P, T], U8, name=name + "_plane", align_bytes=64)
             nc.vector.tensor_copy(plane[:], x_plane[:].indirect(slots[:]))
-            nc.vector.tensor_copy(words[:], x_sb[:].bitcast(U32).indirect(slots[:]))
+            for e in range(E):
+                nc.vector.tensor_copy(
+                    words[:, e * C : (e + 1) * C],
+                    x_sb[:].bitcast(U32).indirect(slots[:, e * C // LIST : (e + 1) * C // LIST]),
+                )
             return words, plane
 
         def project(bank, tag, j, weights, weight_plane, words, plane):
             acc = psum.tile([P, T], F32, name=bank)
             rows = slice(j * P, (j + 1) * P)
+            held = j % (weights.shape[2] // P)
             for e in range(E):
                 cols = slice(e * C, (e + 1) * C)
                 nc.tensor.matmul_mx(
                     out=acc[:, cols],
-                    lhsT=weights[:, e, rows].bitcast(FP8X4),
+                    lhsT=weights[:, e, held * P : (held + 1) * P].bitcast(FP8X4),
                     lhsT_scale=weight_plane[4 * e :, rows],
                     rhs=words[:, cols].bitcast(FP8X4),
                     rhs_scale=plane[:, cols],
@@ -112,6 +132,27 @@ def tile_moe_mlr_relu_kernel(
             by_slot = keep.tile([P, T], F32, name=tag, align_bytes=64)
             nc.scalar.copy(by_slot[:], acc[:])
             return by_slot
+
+        def first_tile_half(e, bank, by_token):
+            cols = slice(e * C, (e + 1) * C)
+            acc = psum.tile([P, C], F32, name=bank)
+            nc.tensor.matmul_mx(
+                out=acc[:],
+                lhsT=w_low[:, e, :P].bitcast(FP8X4),
+                lhsT_scale=w_plane[4 * e :, :P],
+                rhs=xe_words[:, cols].bitcast(FP8X4),
+                rhs_scale=xe_plane[:, cols],
+                start=True,
+                stop=True,
+            )
+            by_slot = keep.tile([P, C], F32, name=f"y_half{e}", align_bytes=64)
+            nc.scalar.copy(by_slot[:], acc[:])
+            nc.vector.tensor_tensor(
+                by_token[:].indirect(expert_list[:, e * C // LIST : (e + 1) * C // LIST]),
+                by_slot[:],
+                gate_sb[:, cols],
+                MULT,
+            )
 
         def scatter(tag, by_slot, weight, slots):
             by_token = keep.tile([P, WINDOW], F32, name=tag, align_bytes=64)
@@ -131,15 +172,18 @@ def tile_moe_mlr_relu_kernel(
                 start=True,
                 stop=True,
             )
-            h_rows = keep.tile([P, PACK, P], BF16, name=f"h_rows{b}", align_bytes=64)
-            nc.scalar.activation(h_rows[:], acc[:].rearrange("m (p d) -> m d p", d=PACK), RELU)
+            h_rows = keep.tile([P, 2, P, 2], BF16, name=f"h_rows{b}", align_bytes=64)
+            nc.scalar.activation(h_rows[:], acc[:].rearrange("m (p u v) -> m u p v", u=2, v=2), RELU)
             return h_rows
 
         def turn_block(b, grouped, h_rows):
-            turned = psum.tile([P, PACK, P], BF16, name="turned", bufs=2)
-            for d in range(PACK):
-                nc.tensor.transpose(turned[:, d, :], h_rows[:, d, :], ident_bf16[:])
-            nc.scalar.copy(grouped[:, b * P : (b + 1) * P, :], turned[:].rearrange("p d m -> p m d"))
+            turned = psum.tile([P, 2, P], F32, name="turned", bufs=2)
+            pairs = h_rows[:].rearrange("m u p v -> m u (p v)").bitcast(F32)
+            for u in range(2):
+                nc.tensor.transpose(turned[:, u, :], pairs[:, u, :], ident_f32[:])
+            nc.scalar.copy(
+                grouped[:, b * P : (b + 1) * P, :].bitcast(F32), turned[:].rearrange("p u m -> p m u")
+            )
 
         def turn_into_sum(sum_t, by_token, first):
             blocks = T // P
@@ -172,15 +216,19 @@ def tile_moe_mlr_relu_kernel(
             nc.scalar.dma_start(out=out[j * P : (j + 1) * P, :], in_=result[:])
 
         xe_words, xe_plane = gather_tokens("xe", expert_list)
-        xa_words, xa_plane = gather_tokens("xa", adapter_list)
+        xa_words = keep.tile([P, T], U32, name="xa_words", align_bytes=64)
+        nc.vector.tensor_copy(xa_words[:], x_sb[:].bitcast(U32).indirect(adapter_list[:]))
 
         def expert_tile(j, bank, tag):
-            return project(bank, tag, j, w_sb, w_plane, xe_words, xe_plane)
+            return project(bank, tag, j, w_low if j < TILES // 2 else w_high, w_plane, xe_words, xe_plane)
 
         def adapter_tile(j):
             return project(f"bank{(j + 2) % 4}", f"z_slots{j}", j, wb_sb, wb_plane, h_words, h_plane)
 
-        o = [scatter(f"y_tokens{j}", expert_tile(j, f"bank{j}", f"y_slots{j}"), gate_sb, expert_list) for j in range(2)]
+        o_first = keep.tile([P, WINDOW], F32, name="y_tokens0", align_bytes=64)
+        first_tile_half(0, "bank0", o_first)
+        o = [o_first, scatter("y_tokens1", expert_tile(1, "bank1", "y_slots1"), gate_sb, expert_list)]
+        first_tile_half(1, "bank1", o_first)
 
         grouped = keep.tile([P, T, PACK], BF16, name="grouped", align_bytes=64)
         h_blocks = [hidden_block(b, grouped, xa_words, xa_plane) for b in range(T // P)]

@@ -71,9 +71,11 @@ def tile_moe_mlr_relu_kernel(
         x_rows = x_scales.bitcast(I32)
         x_spread = keep.tile([P, WINDOW], U8, name="x_spread", align_bytes=64)
         nc.scalar.dma_start(
-            out=x_spread[:, :T].bitcast(I32),
-            in_=x_rows.rearrange("s b w -> b s w").broadcast_to([16, 8, T // 4]),
+            out=x_spread[:32, :T].bitcast(I32),
+            in_=x_rows.rearrange("s b w -> b s w").broadcast_to([16, 2, T // 4]),
         )
+        nc.vector.memset(x_spread[32:64, :T].bitcast(I32), 0)
+        nc.vector.memset(x_spread[64:, :T].bitcast(I32), 0)
         expert_list = load_list("expert_list", offs)
         for q, queue in enumerate((nc.scalar, nc.scalar, nc.sync, nc.sync)):
             queue.dma_start(
@@ -93,7 +95,7 @@ def tile_moe_mlr_relu_kernel(
         for q in range(4):
             nc.sync.dma_start(
                 out=xa_plane[32 * q : 32 * q + 4, :].bitcast(I32),
-                in_=xa_spread[32 * q : 32 * (q + 1) : 8, :].bitcast(I32),
+                in_=xa_spread[8 * q : 8 * (q + 1) : 2, :].bitcast(I32),
             )
         w_high = load_words("w_high", w_words[:, 0, :, N // 2 :])
         load_planes(nc.sync, wb_plane, 0, wb_scales[:, 0])
@@ -228,10 +230,10 @@ def tile_moe_mlr_relu_kernel(
         o_first = keep.tile([P, WINDOW], F32, name="y_tokens0", align_bytes=64)
         first_tile_half(0, "bank0", o_first)
         o = [o_first, scatter("y_tokens1", expert_tile(1, "bank1", "y_slots1"), gate_sb, expert_list)]
-        first_tile_half(1, "bank1", o_first)
 
         grouped = keep.tile([P, T, PACK], BF16, name="grouped", align_bytes=64)
         h_blocks = [hidden_block(b, grouped, xa_words, xa_plane) for b in range(T // P)]
+        first_tile_half(1, "bank2", o_first)
         for b in range(T // P):
             turn_block(b, grouped, h_blocks[b])
         h_words = keep.tile([P, T], U32, name="h_words", align_bytes=64)

@@ -61,21 +61,19 @@ def tile_moe_mlr_relu_kernel(
         planes = {}
         for name in ("w", "wa", "wb"):
             planes[name] = keep.tile([P, T], U8, name=name + "_plane", align_bytes=64)
-            nc.vector.memset(planes[name][:].bitcast(I32), 0)
+            (nc.vector if name == "w" else nc.gpsimd).memset(planes[name][:].bitcast(I32), 0)
         w_plane, wa_plane, wb_plane = planes["w"], planes["wa"], planes["wb"]
 
         xa_plane = keep.tile([P, T], U8, name="xa_plane", align_bytes=64)
-        nc.vector.memset(xa_plane[:].bitcast(I32), 0)
+        nc.gpsimd.memset(xa_plane[:].bitcast(I32), 0)
 
         adapter_list = load_list("adapter_list", offs2)
         x_rows = x_scales.bitcast(I32)
         x_spread = keep.tile([P, WINDOW], U8, name="x_spread", align_bytes=64)
         nc.scalar.dma_start(
-            out=x_spread[:32, :T].bitcast(I32),
-            in_=x_rows.rearrange("s b w -> b s w").broadcast_to([16, 2, T // 4]),
+            out=x_spread[:, :T].bitcast(I32),
+            in_=x_rows.rearrange("s b w -> b s w").broadcast_to([16, 8, T // 4]),
         )
-        nc.vector.memset(x_spread[32:64, :T].bitcast(I32), 0)
-        nc.vector.memset(x_spread[64:, :T].bitcast(I32), 0)
         expert_list = load_list("expert_list", offs)
         for q, queue in enumerate((nc.scalar, nc.scalar, nc.sync, nc.sync)):
             queue.dma_start(
@@ -95,7 +93,7 @@ def tile_moe_mlr_relu_kernel(
         for q in range(4):
             nc.sync.dma_start(
                 out=xa_plane[32 * q : 32 * q + 4, :].bitcast(I32),
-                in_=xa_spread[8 * q : 8 * (q + 1) : 2, :].bitcast(I32),
+                in_=xa_spread[32 * q : 32 * (q + 1) : 8, :].bitcast(I32),
             )
         w_high = load_words("w_high", w_words[:, 0, :, N // 2 :])
         load_planes(nc.sync, wb_plane, 0, wb_scales[:, 0])

@@ -15,6 +15,7 @@ U16 = mybir.dt.uint16
 U8 = mybir.dt.uint8
 FP8X4 = mybir.dt.float8_e4m3fn_x4
 RELU = mybir.ActivationFunctionType.Relu
+COPY = mybir.ActivationFunctionType.Copy
 MULT = mybir.AluOpType.mult
 ADD = mybir.AluOpType.add
 
@@ -22,7 +23,7 @@ P = 128
 PACK = 4
 TILES = N // P
 LIST = 16
-WINDOW = 768
+WIDE = 768
 
 
 def tile_moe_mlr_relu_kernel(
@@ -31,19 +32,20 @@ def tile_moe_mlr_relu_kernel(
     nc = tc.nc
     with ExitStack() as ctx:
         keep = ctx.enter_context(tc.tile_pool(name="keep", bufs=1))
-        stage = ctx.enter_context(tc.tile_pool(name="stage", bufs=2))
         psum = ctx.enter_context(tc.psum_pool(name="psum", bufs=1))
 
-        def load_planes(queue, tile, first_row, scales, quadrants=range(4)):
-            count = scales.shape[0]
+        def sbuf(name, width, dtype):
+            return keep.tile([P, width], dtype, name=name, align_bytes=64)
+
+        def load_planes(tile, scales, quadrants):
             rows = scales.bitcast(I32)
             for q in quadrants:
-                start = 32 * q + first_row
-                queue.dma_start(out=tile[start : start + 4 * count, :T].bitcast(I32), in_=rows[:, 4 * q : 4 * q + 4, :])
+                nc.sync.dma_start(
+                    out=tile[32 * q : 32 * q + 4 * E, :].bitcast(I32), in_=rows[:, 4 * q : 4 * q + 4, :]
+                )
 
         def load_words(name, words):
-            count = words.shape[0]
-            tile = keep.tile([P, count, words.shape[2]], I32, name=name, align_bytes=64)
+            tile = keep.tile([P, words.shape[0], words.shape[2]], I32, name=name, align_bytes=64)
             nc.sync.dma_start(out=tile[:], in_=words.rearrange("e p n d -> p e (n d)").bitcast(I32))
             return tile
 
@@ -53,122 +55,103 @@ def tile_moe_mlr_relu_kernel(
             return tile
 
         def load_gate(name, source):
-            tile = keep.tile([P, T], F32, name=name)
+            tile = sbuf(name, T, F32)
             nc.sync.dma_start(out=tile[:], in_=source)
             return tile
 
-        x_plane = keep.tile([P, WINDOW], U8, name="x_plane", align_bytes=64)
         planes = {}
         for name in ("w", "wa", "wb"):
-            planes[name] = keep.tile([P, T], U8, name=name + "_plane", align_bytes=64)
-            (nc.vector if name == "w" else nc.gpsimd).memset(planes[name][:].bitcast(I32), 0)
+            planes[name] = sbuf(name + "_plane", T, U8)
+            nc.vector.memset(planes[name][:].bitcast(I32), 0)
         w_plane, wa_plane, wb_plane = planes["w"], planes["wa"], planes["wb"]
 
-        xa_plane = keep.tile([P, T], U8, name="xa_plane", align_bytes=64)
-        nc.gpsimd.memset(xa_plane[:].bitcast(I32), 0)
-
-        adapter_list = load_list("adapter_list", offs2)
-        x_rows = x_scales.bitcast(I32)
-        x_spread = keep.tile([P, WINDOW], U8, name="x_spread", align_bytes=64)
-        nc.scalar.dma_start(
-            out=x_spread[:, :T].bitcast(I32),
-            in_=x_rows.rearrange("s b w -> b s w").broadcast_to([16, 8, T // 4]),
-        )
         expert_list = load_list("expert_list", offs)
+        x_rows = x_scales.bitcast(I32)
+        x_plane = sbuf("x_plane", WIDE, U8)
         for q, queue in enumerate((nc.scalar, nc.scalar, nc.sync, nc.sync)):
             queue.dma_start(
                 out=x_plane[32 * q : 32 * (q + 1), :T].bitcast(I32),
                 in_=x_rows[:, 4 * q : 4 * q + 4, :].broadcast_to([8, 4, T // 4]),
             )
-        x_sb = keep.tile([P, WINDOW], I32, name="x_sb", align_bytes=64)
+        x_sb = sbuf("x_sb", WIDE, I32)
         nc.sync.dma_start(out=x_sb[:, :T], in_=x_words[0].rearrange("p t d -> p (t d)").bitcast(I32))
         w_low = load_words("w_low", w_words[:, 0, :, : N // 2])
-        load_planes(nc.sync, w_plane, 0, w_scales[:, 0])
-        load_planes(nc.sync, wa_plane, 8, wa_scales[:, 0], range(1))
+        load_planes(w_plane, w_scales[:, 0], range(4))
         gate_sb = load_gate("gate_sb", gate)
         wa_sb = load_words("wa_sb", wa_words[:, 0])
-        load_planes(nc.sync, wa_plane, 8, wa_scales[:, 0], range(1, 4))
-        xa_spread = keep.tile([P, T], U8, name="xa_spread", align_bytes=64)
-        nc.vector.tensor_copy(xa_spread[:], x_spread[:].indirect(adapter_list[:]))
-        for q in range(4):
-            nc.sync.dma_start(
-                out=xa_plane[32 * q : 32 * q + 4, :].bitcast(I32),
-                in_=xa_spread[32 * q : 32 * (q + 1) : 8, :].bitcast(I32),
-            )
+        adapter_list = load_list("adapter_list", offs2)
+        load_planes(wa_plane, wa_scales[:, 0], range(4))
         w_high = load_words("w_high", w_words[:, 0, :, N // 2 :])
-        load_planes(nc.sync, wb_plane, 0, wb_scales[:, 0])
+        load_planes(wb_plane, wb_scales[:, 0], range(4))
         wb_sb = load_words("wb_sb", wb_words[:, 0])
         gate2_sb = load_gate("gate2_sb", gate2)
 
         ident_f32 = keep.tile([P, P], F32, name="ident_f32")
         make_identity(nc, ident_f32[:])
 
+        def half(e):
+            return slice(e * C, (e + 1) * C)
+
+        def entries(slots, e):
+            return slots[:, e * C // LIST : (e + 1) * C // LIST]
+
         def gather_tokens(name, slots):
-            words = keep.tile([P, T], U32, name=name + "_words", align_bytes=64)
-            plane = keep.tile([P, T], U8, name=name + "_plane", align_bytes=64)
+            plane = sbuf(name + "_plane", T, U8)
             nc.vector.tensor_copy(plane[:], x_plane[:].indirect(slots[:]))
+            words = []
             for e in range(E):
-                nc.vector.tensor_copy(
-                    words[:, e * C : (e + 1) * C],
-                    x_sb[:].bitcast(U32).indirect(slots[:, e * C // LIST : (e + 1) * C // LIST]),
-                )
+                tile = sbuf(f"{name}_words{e}", C, U32)
+                nc.vector.tensor_copy(tile[:], x_sb[:].bitcast(U32).indirect(entries(slots, e)))
+                words.append(tile[:])
             return words, plane
 
-        def project(bank, tag, j, weights, weight_plane, words, plane):
-            acc = psum.tile([P, T], F32, name=bank)
-            rows = slice(j * P, (j + 1) * P)
+        def product(acc, e, j, weights, weight_plane, words, plane):
             held = j % (weights.shape[2] // P)
-            for e in range(E):
-                cols = slice(e * C, (e + 1) * C)
-                nc.tensor.matmul_mx(
-                    out=acc[:, cols],
-                    lhsT=weights[:, e, held * P : (held + 1) * P].bitcast(FP8X4),
-                    lhsT_scale=weight_plane[4 * e :, rows],
-                    rhs=words[:, cols].bitcast(FP8X4),
-                    rhs_scale=plane[:, cols],
-                    start=True,
-                    stop=True,
-                )
-            by_slot = keep.tile([P, T], F32, name=tag, align_bytes=64)
-            nc.scalar.copy(by_slot[:], acc[:])
-            return by_slot
-
-        def first_tile_half(e, bank, by_token):
-            cols = slice(e * C, (e + 1) * C)
-            acc = psum.tile([P, C], F32, name=bank)
             nc.tensor.matmul_mx(
-                out=acc[:],
-                lhsT=w_low[:, e, :P].bitcast(FP8X4),
-                lhsT_scale=w_plane[4 * e :, :P],
-                rhs=xe_words[:, cols].bitcast(FP8X4),
-                rhs_scale=xe_plane[:, cols],
+                out=acc,
+                lhsT=weights[:, e, held * P : (held + 1) * P].bitcast(FP8X4),
+                lhsT_scale=weight_plane[4 * e :, j * P : (j + 1) * P],
+                rhs=words[e].bitcast(FP8X4),
+                rhs_scale=plane[:, half(e)],
                 start=True,
                 stop=True,
             )
-            by_slot = keep.tile([P, C], F32, name=f"y_half{e}", align_bytes=64)
-            nc.scalar.copy(by_slot[:], acc[:])
-            nc.vector.tensor_tensor(
-                by_token[:].indirect(expert_list[:, e * C // LIST : (e + 1) * C // LIST]),
-                by_slot[:],
-                gate_sb[:, cols],
-                MULT,
-            )
 
-        def scatter(tag, by_slot, weight, slots):
-            by_token = keep.tile([P, WINDOW], F32, name=tag, align_bytes=64)
-            nc.vector.tensor_tensor(by_token[:].indirect(slots[:]), by_slot[:], weight[:], MULT)
+        def gated_tile(bank, name, j, weights, weight_plane, words, plane, weight):
+            acc = psum.tile([P, T], F32, name=bank)
+            for e in range(E):
+                product(acc[:, half(e)], e, j, weights, weight_plane, words, plane)
+            by_slot = sbuf(name, T, F32)
+            nc.vector.tensor_tensor(by_slot[:], acc[:], weight[:], MULT)
+            return by_slot
+
+        def scatter_half(engine, by_token, by_slot, slots, e):
+            window = by_token[:].indirect(entries(slots, e))
+            if engine is nc.scalar:
+                nc.scalar.activation(window, by_slot, COPY)
+            else:
+                nc.vector.tensor_copy(window, by_slot)
+
+        def scatter_on_scalar(name, by_slot, slots):
+            by_token = sbuf(name, T, F32)
+            for e in range(E):
+                scatter_half(nc.scalar, by_token, by_slot[:, half(e)], slots, e)
             return by_token
 
-        def hidden_block(b, grouped, words, plane):
-            cols = slice(b * P, (b + 1) * P)
-            f = b * P // C
-            acc = psum.tile([P, H], F32, name=f"bank{(b + 2) % 4}")
+        def scatter_on_vector(name, by_slot, slots):
+            by_token = sbuf(name, WIDE, F32)
+            nc.vector.tensor_copy(by_token[:].indirect(slots[:]), by_slot[:])
+            return by_token
+
+        def hidden_block(b):
+            f, place = divmod(b * P, C)
+            acc = psum.tile([P, H], F32, name=f"bank{2 + b}")
             nc.tensor.matmul_mx(
                 out=acc[:],
-                lhsT=words[:, cols].bitcast(FP8X4),
-                lhsT_scale=plane[:, cols],
+                lhsT=xa_words[f][:, place : place + P].bitcast(FP8X4),
+                lhsT_scale=xa_plane[:, b * P : (b + 1) * P],
                 rhs=wa_sb[:, f, :].bitcast(FP8X4),
-                rhs_scale=wa_plane[8 + 4 * f :, :],
+                rhs_scale=wa_plane[4 * f :, :],
                 start=True,
                 stop=True,
             )
@@ -176,82 +159,76 @@ def tile_moe_mlr_relu_kernel(
             nc.scalar.activation(h_rows[:], acc[:].rearrange("m (p u v) -> m u p v", u=2, v=2), RELU)
             return h_rows
 
-        def turn_block(b, grouped, h_rows):
-            turned = psum.tile([P, 2, P], F32, name="turned", bufs=2)
-            pairs = h_rows[:].rearrange("m u p v -> m u (p v)").bitcast(F32)
-            for u in range(2):
-                nc.tensor.transpose(turned[:, u, :], pairs[:, u, :], ident_f32[:])
+        def turn_blocks(f, blocks):
+            turned = psum.tile([P, 2, 2, P], F32, name=f"bank{f}")
+            for b, h_rows in enumerate(blocks):
+                pairs = h_rows[:].rearrange("m u p v -> m u (p v)").bitcast(F32)
+                for u in range(2):
+                    nc.tensor.transpose(turned[:, b, u, :], pairs[:, u, :], ident_f32[:])
             nc.scalar.copy(
-                grouped[:, b * P : (b + 1) * P, :].bitcast(F32), turned[:].rearrange("p u m -> p m u")
+                grouped[:, half(f), :].bitcast(F32).rearrange("p (b m) u -> p b m u", b=2),
+                turned[:].rearrange("p b u m -> p b m u"),
             )
 
-        def turn_into_sum(sum_t, by_token, first):
-            blocks = T // P
-            for b in range(blocks):
-                cols = slice(b * P, (b + 1) * P)
-                nc.tensor.matmul(
-                    sum_t[:, cols],
-                    by_token[:, cols],
-                    ident_f32[:],
-                    start=first and b == 0,
-                    stop=not first and b == blocks - 1,
-                    is_transpose=True,
-                )
-
-        def open_sum(j, o_tokens):
-            sum_t = psum.tile([P, T], F32, name=f"bank{(j + 2) % 4}")
-            turn_into_sum(sum_t, o_tokens, True)
-            return sum_t
-
-        def close_sum(j, sum_t, z_tokens):
-            turn_into_sum(sum_t, z_tokens, False)
-            sum_t_sb = stage.tile([P, T], F32, name="sum_t_sb")
-            nc.scalar.copy(sum_t_sb[:], sum_t[:])
-            back = psum.tile([P, T], F32, name="turned", bufs=2)
-            for b in range(T // P):
-                cols = slice(b * P, (b + 1) * P)
-                nc.tensor.transpose(back[:, cols], sum_t_sb[:, cols], ident_f32[:])
-            result = stage.tile([P, T], F32, name="result")
-            nc.scalar.copy(result[:], back[:])
-            nc.scalar.dma_start(out=out[j * P : (j + 1) * P, :], in_=result[:])
+        def add_and_store(j, o_tokens, z_tokens):
+            result = sbuf(f"result{j}", T, F32)
+            nc.gpsimd.tensor_tensor(result[:], o_tokens[:, :T], z_tokens[:, :T], ADD)
+            nc.sync.dma_start(out=out[j * P : (j + 1) * P, :], in_=result[:])
 
         xe_words, xe_plane = gather_tokens("xe", expert_list)
-        xa_words = keep.tile([P, T], U32, name="xa_words", align_bytes=64)
-        nc.vector.tensor_copy(xa_words[:], x_sb[:].bitcast(U32).indirect(adapter_list[:]))
+        o = [sbuf("y_tokens0", T, F32)]
+        for e in range(E):
+            acc = psum.tile([P, C], F32, name=f"bank{e}")
+            product(acc[:], e, 0, w_low, w_plane, xe_words, xe_plane)
+            by_slot = sbuf(f"y_half{e}", C, F32)
+            nc.vector.tensor_tensor(by_slot[:], acc[:], gate_sb[:, half(e)], MULT)
+            scatter_half(nc.scalar, o[0], by_slot[:], expert_list, e)
 
-        def expert_tile(j, bank, tag):
-            return project(bank, tag, j, w_low if j < TILES // 2 else w_high, w_plane, xe_words, xe_plane)
+        def expert_tile(j, bank):
+            weights = w_low if j < TILES // 2 else w_high
+            return gated_tile(bank, f"y_slots{j}", j, weights, w_plane, xe_words, xe_plane, gate_sb)
 
-        def adapter_tile(j):
-            return project(f"bank{(j + 2) % 4}", f"z_slots{j}", j, wb_sb, wb_plane, h_words, h_plane)
+        def adapter_tile(j, bank):
+            return gated_tile(bank, f"z_slots{j}", j, wb_sb, wb_plane, h_halves, h_plane, gate2_sb)
 
-        o_first = keep.tile([P, WINDOW], F32, name="y_tokens0", align_bytes=64)
-        first_tile_half(0, "bank0", o_first)
-        o = [o_first, scatter("y_tokens1", expert_tile(1, "bank1", "y_slots1"), gate_sb, expert_list)]
+        y1 = expert_tile(1, "bank6")
+        xa_words, xa_plane = gather_tokens("xa", adapter_list)
+        o.append(scatter_on_vector("x_sb", y1, expert_list))
 
         grouped = keep.tile([P, T, PACK], BF16, name="grouped", align_bytes=64)
-        h_blocks = [hidden_block(b, grouped, xa_words, xa_plane) for b in range(T // P)]
-        first_tile_half(1, "bank2", o_first)
-        for b in range(T // P):
-            turn_block(b, grouped, h_blocks[b])
-        h_words = keep.tile([P, T], U32, name="h_words", align_bytes=64)
-        h_plane = keep.tile([P, T], U8, name="h_plane", align_bytes=64)
+        h_blocks = [hidden_block(b) for b in range(T // P)]
+        for f in range(E):
+            turn_blocks(f, h_blocks[2 * f : 2 * f + 2])
+
+        y2 = expert_tile(2, "bank4")
+        o.append(scatter_on_scalar("y_tokens2", y2, expert_list))
+
+        h_words = sbuf("h_words", T, U32)
+        h_plane = sbuf("h_plane", T, U8)
         nc.vector.quantize_mx(
             out=h_words[:].bitcast(FP8X4), scales=h_plane[:], in_=grouped[:].rearrange("p m d -> p (m d)")
         )
+        h_halves = [h_words[:, half(e)] for e in range(E)]
 
+        y3 = expert_tile(3, "bank1")
+        z1 = adapter_tile(1, "bank0")
+        z2 = adapter_tile(2, "bank6")
+        z3 = adapter_tile(3, "bank7")
+        z0 = adapter_tile(0, "bank2")
+
+        z1_tokens = scatter_on_scalar("z_tokens1", z1, adapter_list)
+        z2_tokens = sbuf("z_tokens2", T, F32)
+        scatter_half(nc.vector, z2_tokens, z2[:, half(0)], adapter_list, 0)
+        z0_tokens = scatter_on_vector("z_tokens0", z0, adapter_list)
+        scatter_half(nc.scalar, z2_tokens, z2[:, half(1)], adapter_list, 1)
+        z3_tokens = scatter_on_scalar("z_slots2", z3, adapter_list)
+        o.append(scatter_on_vector("gate2_sb", y3, expert_list))
+
+        add_and_store(1, o[1], z1_tokens)
+        add_and_store(2, o[2], z2_tokens)
+        add_and_store(0, o[0], z0_tokens)
         last = TILES - 1
-        o.append(scatter("y_tokens2", expert_tile(2, "bank4", "h_rows3"), gate_sb, expert_list))
-        z = [adapter_tile(j) for j in range(TILES)]
-        y_last = expert_tile(last, "bank5", "grouped")
-        sums = [open_sum(j, o[j]) for j in range(last)]
-        for j in range(last):
-            close_sum(j, sums[j], scatter(f"z_tokens{j}", z[j], gate2_sb, adapter_list))
-
-        o_last = scatter("z_slots1", y_last, gate_sb, expert_list)
-        z_last = scatter("z_tokens3", z[last], gate2_sb, adapter_list)
-        final = keep.tile([P, T], F32, name="final")
-        half = T // 2
-        for cols in (slice(0, half), slice(half, T)):
-            nc.vector.tensor_tensor(final[:, cols], o_last[:, cols], z_last[:, cols], ADD)
-            nc.sync.dma_start(out=out[last * P :, cols], in_=final[:, cols])
+        final = sbuf("final", T, F32)
+        for e in range(2):
+            nc.vector.tensor_tensor(final[:, half(e)], o[last][:, half(e)], z3_tokens[:, half(e)], ADD)
+            nc.sync.dma_start(out=out[last * P :, half(e)], in_=final[:, half(e)])

@@ -24,6 +24,7 @@ PACK = 4
 TILES = N // P
 LIST = 16
 WIDE = 768
+SHARE = 160
 
 
 def tile_moe_mlr_relu_kernel(
@@ -73,17 +74,20 @@ def tile_moe_mlr_relu_kernel(
                 out=x_plane[32 * q : 32 * (q + 1), :T].bitcast(I32),
                 in_=x_rows[:, 4 * q : 4 * q + 4, :].broadcast_to([8, 4, T // 4]),
             )
-        x_sb = sbuf("x_sb", WIDE, I32)
-        nc.sync.dma_start(out=x_sb[:, :T], in_=x_words[0].rearrange("p t d -> p (t d)").bitcast(I32))
-        w_low = load_words("w_low", w_words[:, 0, :, : N // 2])
+        x_sb = sbuf("x_sb", T, I32)
+        nc.sync.dma_start(out=x_sb[:], in_=x_words[0].rearrange("p t d -> p (t d)").bitcast(I32))
+        w_sb = [load_words("w_first", w_words[0])]
         load_planes(w_plane, w_scales[:, 0], range(4))
         gate_sb = load_gate("gate_sb", gate)
-        wa_sb = load_words("wa_sb", wa_words[:, 0])
+        w_sb.append(load_words("w_second", w_words[1]))
+        wa_sb = [load_words("wa_first", wa_words[0])]
         adapter_list = load_list("adapter_list", offs2)
         load_planes(wa_plane, wa_scales[:, 0], range(4))
-        w_high = load_words("w_high", w_words[:, 0, :, N // 2 :])
+        wa_sb.append(load_words("wa_second", wa_words[1]))
         load_planes(wb_plane, wb_scales[:, 0], range(4))
-        wb_sb = load_words("wb_sb", wb_words[:, 0])
+        wb_both = load_words("wb_sb", wb_words[:, 0])
+        wb_sb = [wb_both[:, f, :] for f in range(E)]
+        w_sb = [tile[:, 0, :] for tile in w_sb]
         gate2_sb = load_gate("gate2_sb", gate2)
 
         ident_f32 = keep.tile([P, P], F32, name="ident_f32")
@@ -95,21 +99,20 @@ def tile_moe_mlr_relu_kernel(
         def entries(slots, e):
             return slots[:, e * C // LIST : (e + 1) * C // LIST]
 
-        def gather_tokens(name, slots):
-            plane = sbuf(name + "_plane", T, U8)
-            nc.vector.tensor_copy(plane[:], x_plane[:].indirect(slots[:]))
-            words = []
-            for e in range(E):
-                tile = sbuf(f"{name}_words{e}", C, U32)
-                nc.vector.tensor_copy(tile[:], x_sb[:].bitcast(U32).indirect(entries(slots, e)))
-                words.append(tile[:])
-            return words, plane
+        def gather_words(name, slots, e):
+            tile = sbuf(name, C, U32)
+            nc.vector.tensor_copy(tile[:], x_sb[:].bitcast(U32).indirect(entries(slots, e)))
+            return tile[:]
 
-        def product(acc, e, j, weights, weight_plane, words, plane):
-            held = j % (weights.shape[2] // P)
+        def gather_plane(name, offsets):
+            tile = sbuf(name, offsets.shape[1] * LIST, U8)
+            nc.vector.tensor_copy(tile[:], x_plane[:].indirect(offsets))
+            return tile[:]
+
+        def product(acc, j, e, weights, weight_plane, words, plane):
             nc.tensor.matmul_mx(
                 out=acc,
-                lhsT=weights[:, e, held * P : (held + 1) * P].bitcast(FP8X4),
+                lhsT=weights[e][:, j * P : (j + 1) * P].bitcast(FP8X4),
                 lhsT_scale=weight_plane[4 * e :, j * P : (j + 1) * P],
                 rhs=words[e].bitcast(FP8X4),
                 rhs_scale=plane[:, half(e)],
@@ -117,30 +120,25 @@ def tile_moe_mlr_relu_kernel(
                 stop=True,
             )
 
-        def gated_tile(bank, name, j, weights, weight_plane, words, plane, weight):
-            acc = psum.tile([P, T], F32, name=bank)
-            for e in range(E):
-                product(acc[:, half(e)], e, j, weights, weight_plane, words, plane)
-            by_slot = sbuf(name, T, F32)
-            nc.vector.tensor_tensor(by_slot[:], acc[:], weight[:], MULT)
+        def gated_pair(bank, name, pieces, weights, weight_plane, words, plane, weight):
+            acc = psum.tile([P, 2, C], F32, name=bank)
+            for place, (j, e) in enumerate(pieces):
+                product(acc[:, place, :], j, e, weights, weight_plane, words, plane)
+            e0, e1 = pieces[0][1], pieces[1][1]
+            if e0 == e1:
+                factor = weight[:, half(e0)].unsqueeze(1).broadcast_to([P, 2, C])
+            else:
+                factor = weight[:].rearrange("p (e c) -> p e c", e=E)
+            by_slot = keep.tile([P, 2, C], F32, name=name, align_bytes=64)
+            nc.vector.tensor_tensor(by_slot[:], acc[:], factor, MULT)
             return by_slot
 
-        def scatter_half(engine, by_token, by_slot, slots, e):
-            window = by_token[:].indirect(entries(slots, e))
-            if engine is nc.scalar:
-                nc.scalar.activation(window, by_slot, COPY)
-            else:
-                nc.vector.tensor_copy(window, by_slot)
-
-        def scatter_on_scalar(name, by_slot, slots):
-            by_token = sbuf(name, T, F32)
-            for e in range(E):
-                scatter_half(nc.scalar, by_token, by_slot[:, half(e)], slots, e)
-            return by_token
+        def scatter_half(by_token, by_slot, slots, e):
+            nc.scalar.activation(by_token[:].indirect(entries(slots, e)), by_slot, COPY)
 
         def scatter_on_vector(name, by_slot, slots):
             by_token = sbuf(name, WIDE, F32)
-            nc.vector.tensor_copy(by_token[:].indirect(slots[:]), by_slot[:])
+            nc.vector.tensor_copy(by_token[:].indirect(slots[:]), by_slot[:].rearrange("p e c -> p (e c)"))
             return by_token
 
         def hidden_block(b):
@@ -149,8 +147,8 @@ def tile_moe_mlr_relu_kernel(
             nc.tensor.matmul_mx(
                 out=acc[:],
                 lhsT=xa_words[f][:, place : place + P].bitcast(FP8X4),
-                lhsT_scale=xa_plane[:, b * P : (b + 1) * P],
-                rhs=wa_sb[:, f, :].bitcast(FP8X4),
+                lhsT_scale=xa_planes[f][:, place : place + P],
+                rhs=wa_sb[f][:, 0, :].bitcast(FP8X4),
                 rhs_scale=wa_plane[4 * f :, :],
                 start=True,
                 stop=True,
@@ -170,65 +168,91 @@ def tile_moe_mlr_relu_kernel(
                 turned[:].rearrange("p b u m -> p b m u"),
             )
 
-        def add_and_store(j, o_tokens, z_tokens):
-            result = sbuf(f"result{j}", T, F32)
+        def add_and_store(name, j, o_tokens, z_tokens):
+            result = sbuf(name, T, F32)
             nc.gpsimd.tensor_tensor(result[:], o_tokens[:, :T], z_tokens[:, :T], ADD)
             nc.sync.dma_start(out=out[j * P : (j + 1) * P, :], in_=result[:])
 
-        xe_words, xe_plane = gather_tokens("xe", expert_list)
-        o = [sbuf("y_tokens0", T, F32)]
+        def expert_pair(bank, name, pieces):
+            return gated_pair(bank, name, pieces, w_sb, w_plane, xe_words, xe_plane, gate_sb)
+
+        def adapter_pair(bank, name, pieces):
+            return gated_pair(bank, name, pieces, wb_sb, wb_plane, h_halves, h_plane, gate2_sb)
+
+        def gated_half(name, acc, e):
+            by_slot = sbuf(name, C, F32)
+            nc.vector.tensor_tensor(by_slot[:], acc, gate_sb[:, half(e)], MULT)
+            return by_slot[:]
+
+        def expert_half(bank, name, j, e):
+            acc = psum.tile([P, C], F32, name=bank)
+            product(acc[:], j, e, w_sb, w_plane, xe_words, xe_plane)
+            return gated_half(name, acc[:], e)
+
+        xe_plane = gather_plane("xe_plane", expert_list[:])
+        xe_words = [gather_words(f"xe_words{e}", expert_list, e) for e in range(E)]
+        y0_tokens = sbuf("y_tokens0", T, F32)
+        y2_tokens = sbuf("y_tokens2", T, F32)
+        scatter_half(y0_tokens, expert_half("bank0", "y_first0", 0, 0), expert_list, 0)
+        scatter_half(y2_tokens, expert_half("bank1", "y_first2", 2, 0), expert_list, 0)
+
+        y1_sums = psum.tile([P, T], F32, name="bank6")
         for e in range(E):
-            acc = psum.tile([P, C], F32, name=f"bank{e}")
-            product(acc[:], e, 0, w_low, w_plane, xe_words, xe_plane)
-            by_slot = sbuf(f"y_half{e}", C, F32)
-            nc.vector.tensor_tensor(by_slot[:], acc[:], gate_sb[:, half(e)], MULT)
-            scatter_half(nc.scalar, o[0], by_slot[:], expert_list, e)
-
-        def expert_tile(j, bank):
-            weights = w_low if j < TILES // 2 else w_high
-            return gated_tile(bank, f"y_slots{j}", j, weights, w_plane, xe_words, xe_plane, gate_sb)
-
-        def adapter_tile(j, bank):
-            return gated_tile(bank, f"z_slots{j}", j, wb_sb, wb_plane, h_halves, h_plane, gate2_sb)
-
-        y1 = expert_tile(1, "bank6")
-        xa_words, xa_plane = gather_tokens("xa", adapter_list)
-        o.append(scatter_on_vector("x_sb", y1, expert_list))
+            product(y1_sums[:, half(e)], 1, e, w_sb, w_plane, xe_words, xe_plane)
+        xa_planes = [gather_plane("xa_plane0", entries(adapter_list, 0))]
+        xa_words = [gather_words("xa_words0", adapter_list, 0)]
+        y1_first = gated_half("y_first1", y1_sums[:, half(0)], 0)
+        xa_planes.append(gather_plane("xa_plane1", entries(adapter_list, 1)))
+        xa_words.append(gather_words("xa_words1", adapter_list, 1))
+        y1_tokens = sbuf("x_plane", T, F32)
+        nc.vector.tensor_copy(y1_tokens[:].indirect(entries(expert_list, 0)), y1_first)
 
         grouped = keep.tile([P, T, PACK], BF16, name="grouped", align_bytes=64)
         h_blocks = [hidden_block(b) for b in range(T // P)]
         for f in range(E):
             turn_blocks(f, h_blocks[2 * f : 2 * f + 2])
 
-        y2 = expert_tile(2, "bank4")
-        o.append(scatter_on_scalar("y_tokens2", y2, expert_list))
+        y1_second = gated_half("xa_words1", y1_sums[:, half(1)], 1)
+        y_second = expert_pair("bank7", "wa_second", [(0, 1), (2, 1)])
+        nc.vector.tensor_copy(y1_tokens[:].indirect(entries(expert_list, 1)), y1_second)
+        scatter_half(y0_tokens, y_second[:, 0, :], expert_list, 1)
+        scatter_half(y2_tokens, y_second[:, 1, :], expert_list, 1)
 
         h_words = sbuf("h_words", T, U32)
         h_plane = sbuf("h_plane", T, U8)
-        nc.vector.quantize_mx(
-            out=h_words[:].bitcast(FP8X4), scales=h_plane[:], in_=grouped[:].rearrange("p m d -> p (m d)")
-        )
         h_halves = [h_words[:, half(e)] for e in range(E)]
 
-        y3 = expert_tile(3, "bank1")
-        z1 = adapter_tile(1, "bank0")
-        z2 = adapter_tile(2, "bank6")
-        z3 = adapter_tile(3, "bank7")
-        z0 = adapter_tile(0, "bank2")
+        def quantise(f):
+            nc.vector.quantize_mx(
+                out=h_halves[f].bitcast(FP8X4),
+                scales=h_plane[:, half(f)],
+                in_=grouped[:, half(f), :].rearrange("p m d -> p (m d)"),
+            )
 
-        z1_tokens = scatter_on_scalar("z_tokens1", z1, adapter_list)
+        quantise(0)
+        y3 = expert_pair("bank0", "y_slots3", [(3, 0), (3, 1)])
+        quantise(1)
+        z_first = adapter_pair("bank2", "z_first", [(1, 0), (2, 0)])
+        z_second = adapter_pair("bank6", "z_second", [(1, 1), (2, 1)])
+        z0 = adapter_pair("bank1", "z_slots0", [(0, 0), (0, 1)])
+        z3 = adapter_pair("bank3", "z_slots3", [(3, 0), (3, 1)])[:].rearrange("p e c -> p (e c)")
+
+        z1_tokens = sbuf("z_tokens1", T, F32)
         z2_tokens = sbuf("z_tokens2", T, F32)
-        scatter_half(nc.vector, z2_tokens, z2[:, half(0)], adapter_list, 0)
-        z0_tokens = scatter_on_vector("z_tokens0", z0, adapter_list)
-        scatter_half(nc.scalar, z2_tokens, z2[:, half(1)], adapter_list, 1)
-        z3_tokens = scatter_on_scalar("z_slots2", z3, adapter_list)
-        o.append(scatter_on_vector("gate2_sb", y3, expert_list))
+        z3_tokens = sbuf("z_tokens3", T, F32)
+        for e, pair in enumerate((z_first, z_second)):
+            scatter_half(z1_tokens, pair[:, 0, :], adapter_list, e)
+            scatter_half(z2_tokens, pair[:, 1, :], adapter_list, e)
+        z0_tokens = scatter_on_vector("wb_sb", z0, adapter_list)
+        nc.vector.tensor_copy(z3_tokens[:].indirect(adapter_list[:, : SHARE // LIST]), z3[:, :SHARE])
+        nc.scalar.activation(z3_tokens[:].indirect(adapter_list[:, SHARE // LIST :]), z3[:, SHARE:], COPY)
+        y3_tokens = scatter_on_vector("gate2_sb", y3, expert_list)
 
-        add_and_store(1, o[1], z1_tokens)
-        add_and_store(2, o[2], z2_tokens)
-        add_and_store(0, o[0], z0_tokens)
+        add_and_store("result0", 0, y0_tokens, z0_tokens)
+        add_and_store("wb_sb", 1, y1_tokens, z1_tokens)
+        add_and_store("z_tokens1", 2, y2_tokens, z2_tokens)
         last = TILES - 1
-        final = sbuf("final", T, F32)
+        final = sbuf("z_tokens2", T, F32)
         for e in range(2):
-            nc.vector.tensor_tensor(final[:, half(e)], o[last][:, half(e)], z3_tokens[:, half(e)], ADD)
+            nc.vector.tensor_tensor(final[:, half(e)], y3_tokens[:, half(e)], z3_tokens[:, half(e)], ADD)
             nc.sync.dma_start(out=out[last * P :, half(e)], in_=final[:, half(e)])

@@ -1,7 +1,6 @@
 from contextlib import ExitStack
 
 import concourse.mybir as mybir
-from concourse.masks import make_identity
 
 K, T, N, H = 512, 512, 512, 512
 E, C = 2, 256
@@ -24,7 +23,7 @@ PACK = 4
 TILES = N // P
 LIST = 16
 WIDE = 768
-SHARE = 160
+SHARE = 128
 
 
 def tile_moe_mlr_relu_kernel(
@@ -79,10 +78,11 @@ def tile_moe_mlr_relu_kernel(
         w_sb = [load_words("w_first", w_words[0])]
         load_planes(w_plane, w_scales[:, 0], range(4))
         gate_sb = load_gate("gate_sb", gate)
-        w_sb.append(load_words("w_second", w_words[1]))
         wa_sb = [load_words("wa_first", wa_words[0])]
+        load_planes(wa_plane, wa_scales[:, 0], range(2))
         adapter_list = load_list("adapter_list", offs2)
-        load_planes(wa_plane, wa_scales[:, 0], range(4))
+        load_planes(wa_plane, wa_scales[:, 0], range(2, 4))
+        w_sb.append(load_words("w_second", w_words[1]))
         wa_sb.append(load_words("wa_second", wa_words[1]))
         load_planes(wb_plane, wb_scales[:, 0], range(4))
         wb_both = load_words("wb_sb", wb_words[:, 0])
@@ -90,8 +90,14 @@ def tile_moe_mlr_relu_kernel(
         w_sb = [tile[:, 0, :] for tile in w_sb]
         gate2_sb = load_gate("gate2_sb", gate2)
 
-        ident_f32 = keep.tile([P, P], F32, name="ident_f32")
-        make_identity(nc, ident_f32[:])
+        def columns_by_place(name, source, dtype):
+            tile = keep.tile([P, PACK, P], dtype, name=name, align_bytes=64)
+            nc.gpsimd.tensor_copy(tile[:], source.rearrange("p (m t) -> p t m", t=PACK))
+            return tile
+
+        wa_placed = [columns_by_place("wa_placed0", wa_sb[0][:, 0, :], I32)]
+        wa_plane_placed = columns_by_place("wa_plane_placed", wa_plane[:], U8)
+        wa_placed.append(columns_by_place("wa_placed1", wa_sb[1][:, 0, :], I32))
 
         def half(e):
             return slice(e * C, (e + 1) * C)
@@ -143,29 +149,21 @@ def tile_moe_mlr_relu_kernel(
 
         def hidden_block(b):
             f, place = divmod(b * P, C)
-            acc = psum.tile([P, H], F32, name=f"bank{2 + b}")
-            nc.tensor.matmul_mx(
-                out=acc[:],
-                lhsT=xa_words[f][:, place : place + P].bitcast(FP8X4),
-                lhsT_scale=xa_planes[f][:, place : place + P],
-                rhs=wa_sb[f][:, 0, :].bitcast(FP8X4),
-                rhs_scale=wa_plane[4 * f :, :],
-                start=True,
-                stop=True,
-            )
-            h_rows = keep.tile([P, 2, P, 2], BF16, name=f"h_rows{b}", align_bytes=64)
-            nc.scalar.activation(h_rows[:], acc[:].rearrange("m (p u v) -> m u p v", u=2, v=2), RELU)
-            return h_rows
-
-        def turn_blocks(f, blocks):
-            turned = psum.tile([P, 2, 2, P], F32, name=f"bank{f}")
-            for b, h_rows in enumerate(blocks):
-                pairs = h_rows[:].rearrange("m u p v -> m u (p v)").bitcast(F32)
-                for u in range(2):
-                    nc.tensor.transpose(turned[:, b, u, :], pairs[:, u, :], ident_f32[:])
-            nc.scalar.copy(
-                grouped[:, half(f), :].bitcast(F32).rearrange("p (b m) u -> p b m u", b=2),
-                turned[:].rearrange("p b u m -> p b m u"),
+            acc = psum.tile([P, PACK, P], F32, name=f"bank{2 + b}")
+            for t in range(PACK):
+                nc.tensor.matmul_mx(
+                    out=acc[:, t, :],
+                    lhsT=wa_placed[f][:, t, :].bitcast(FP8X4),
+                    lhsT_scale=wa_plane_placed[4 * f :, t, :],
+                    rhs=xa_words[f][:, place : place + P].bitcast(FP8X4),
+                    rhs_scale=xa_planes[f][:, place : place + P],
+                    start=True,
+                    stop=True,
+                )
+            nc.scalar.activation(
+                grouped[:, b * P : (b + 1) * P, :].rearrange("p (c i) t -> p c t i", i=2),
+                acc[:].rearrange("p t (c i) -> p c t i", i=2),
+                RELU,
             )
 
         def add_and_store(name, j, o_tokens, z_tokens):
@@ -208,33 +206,25 @@ def tile_moe_mlr_relu_kernel(
         nc.vector.tensor_copy(y1_tokens[:].indirect(entries(expert_list, 0)), y1_first)
 
         grouped = keep.tile([P, T, PACK], BF16, name="grouped", align_bytes=64)
-        h_blocks = [hidden_block(b) for b in range(T // P)]
-        for f in range(E):
-            turn_blocks(f, h_blocks[2 * f : 2 * f + 2])
+        for b in range(T // P):
+            hidden_block(b)
 
+        y_second = expert_pair("bank7", "wa_placed1", [(0, 1), (2, 1)])
         y1_second = gated_half("xa_words1", y1_sums[:, half(1)], 1)
-        y_second = expert_pair("bank7", "wa_second", [(0, 1), (2, 1)])
-        nc.vector.tensor_copy(y1_tokens[:].indirect(entries(expert_list, 1)), y1_second)
         scatter_half(y0_tokens, y_second[:, 0, :], expert_list, 1)
         scatter_half(y2_tokens, y_second[:, 1, :], expert_list, 1)
 
         h_words = sbuf("h_words", T, U32)
         h_plane = sbuf("h_plane", T, U8)
         h_halves = [h_words[:, half(e)] for e in range(E)]
-
-        def quantise(f):
-            nc.vector.quantize_mx(
-                out=h_halves[f].bitcast(FP8X4),
-                scales=h_plane[:, half(f)],
-                in_=grouped[:, half(f), :].rearrange("p m d -> p (m d)"),
-            )
-
-        quantise(0)
-        y3 = expert_pair("bank0", "y_slots3", [(3, 0), (3, 1)])
-        quantise(1)
-        z_first = adapter_pair("bank2", "z_first", [(1, 0), (2, 0)])
+        nc.vector.quantize_mx(
+            out=h_words[:].bitcast(FP8X4), scales=h_plane[:], in_=grouped[:].rearrange("p m d -> p (m d)")
+        )
+        nc.vector.tensor_copy(y1_tokens[:].indirect(entries(expert_list, 1)), y1_second)
+        z_first = adapter_pair("bank1", "z_first", [(1, 0), (2, 0)])
+        y3 = expert_pair("bank5", "y_slots3", [(3, 0), (3, 1)])
         z_second = adapter_pair("bank6", "z_second", [(1, 1), (2, 1)])
-        z0 = adapter_pair("bank1", "z_slots0", [(0, 0), (0, 1)])
+        z0 = adapter_pair("bank2", "z_slots0", [(0, 0), (0, 1)])
         z3 = adapter_pair("bank3", "z_slots3", [(3, 0), (3, 1)])[:].rearrange("p e c -> p (e c)")
 
         z1_tokens = sbuf("z_tokens1", T, F32)

@@ -23,7 +23,7 @@ PACK = 4
 TILES = N // P
 LIST = 16
 WIDE = 768
-SHARE = 128
+SHARE = 192
 
 
 def tile_moe_mlr_relu_kernel(
@@ -77,13 +77,15 @@ def tile_moe_mlr_relu_kernel(
         nc.sync.dma_start(out=x_sb[:], in_=x_words[0].rearrange("p t d -> p (t d)").bitcast(I32))
         w_sb = [load_words("w_first", w_words[0])]
         load_planes(w_plane, w_scales[:, 0], range(4))
-        gate_sb = load_gate("gate_sb", gate)
+        gate_sb = sbuf("gate_sb", T, F32)
+        nc.sync.dma_start(out=gate_sb[:, :C], in_=gate[:, :C])
         wa_sb = [load_words("wa_first", wa_words[0])]
         load_planes(wa_plane, wa_scales[:, 0], range(2))
         adapter_list = load_list("adapter_list", offs2)
         load_planes(wa_plane, wa_scales[:, 0], range(2, 4))
         w_sb.append(load_words("w_second", w_words[1]))
         wa_sb.append(load_words("wa_second", wa_words[1]))
+        nc.sync.dma_start(out=gate_sb[:, C:], in_=gate[:, C:])
         load_planes(wb_plane, wb_scales[:, 0], range(4))
         wb_both = load_words("wb_sb", wb_words[:, 0])
         wb_sb = [wb_both[:, f, :] for f in range(E)]
@@ -221,25 +223,30 @@ def tile_moe_mlr_relu_kernel(
             out=h_words[:].bitcast(FP8X4), scales=h_plane[:], in_=grouped[:].rearrange("p m d -> p (m d)")
         )
         nc.vector.tensor_copy(y1_tokens[:].indirect(entries(expert_list, 1)), y1_second)
+        z0_sums = psum.tile([P, T], F32, name="bank2")
+        for f in range(E):
+            product(z0_sums[:, half(f)], 0, f, wb_sb, wb_plane, h_halves, h_plane)
+        z0 = sbuf("z_slots0", T, F32)
+        nc.scalar.copy(z0[:], z0_sums[:])
         z_first = adapter_pair("bank1", "z_first", [(1, 0), (2, 0)])
-        y3 = expert_pair("bank5", "y_slots3", [(3, 0), (3, 1)])
-        z_second = adapter_pair("bank6", "z_second", [(1, 1), (2, 1)])
-        z0 = adapter_pair("bank2", "z_slots0", [(0, 0), (0, 1)])
         z3 = adapter_pair("bank3", "z_slots3", [(3, 0), (3, 1)])[:].rearrange("p e c -> p (e c)")
+        z_second = adapter_pair("bank4", "z_second", [(1, 1), (2, 1)])
+        y3 = expert_pair("bank1", "y_slots3", [(3, 0), (3, 1)])
 
         z1_tokens = sbuf("z_tokens1", T, F32)
         z2_tokens = sbuf("z_tokens2", T, F32)
-        z3_tokens = sbuf("z_tokens3", T, F32)
         for e, pair in enumerate((z_first, z_second)):
             scatter_half(z1_tokens, pair[:, 0, :], adapter_list, e)
             scatter_half(z2_tokens, pair[:, 1, :], adapter_list, e)
-        z0_tokens = scatter_on_vector("wb_sb", z0, adapter_list)
+        z0_tokens = sbuf("w_second", WIDE, F32)
+        nc.vector.tensor_tensor(z0_tokens[:].indirect(adapter_list[:]), z0[:], gate2_sb[:], MULT)
+        z3_tokens = sbuf("gate_sb", T, F32)
         nc.vector.tensor_copy(z3_tokens[:].indirect(adapter_list[:, : SHARE // LIST]), z3[:, :SHARE])
         nc.scalar.activation(z3_tokens[:].indirect(adapter_list[:, SHARE // LIST :]), z3[:, SHARE:], COPY)
-        y3_tokens = scatter_on_vector("gate2_sb", y3, expert_list)
+        y3_tokens = scatter_on_vector("y_tokens3", y3, expert_list)
 
         add_and_store("result0", 0, y0_tokens, z0_tokens)
-        add_and_store("wb_sb", 1, y1_tokens, z1_tokens)
+        add_and_store("w_second", 1, y1_tokens, z1_tokens)
         add_and_store("z_tokens1", 2, y2_tokens, z2_tokens)
         last = TILES - 1
         final = sbuf("z_tokens2", T, F32)

@@ -23,7 +23,7 @@ PACK = 4
 TILES = N // P
 LIST = 16
 WIDE = 768
-SHARE = 192
+SHARE = 256
 
 
 def tile_moe_mlr_relu_kernel(
@@ -82,8 +82,8 @@ def tile_moe_mlr_relu_kernel(
         wa_sb = [load_words("wa_first", wa_words[0])]
         load_planes(wa_plane, wa_scales[:, 0], range(2))
         adapter_list = load_list("adapter_list", offs2)
-        load_planes(wa_plane, wa_scales[:, 0], range(2, 4))
         w_sb.append(load_words("w_second", w_words[1]))
+        load_planes(wa_plane, wa_scales[:, 0], range(2, 4))
         wa_sb.append(load_words("wa_second", wa_words[1]))
         nc.sync.dma_start(out=gate_sb[:, C:], in_=gate[:, C:])
         load_planes(wb_plane, wb_scales[:, 0], range(4))
@@ -193,26 +193,51 @@ def tile_moe_mlr_relu_kernel(
         xe_words = [gather_words(f"xe_words{e}", expert_list, e) for e in range(E)]
         y0_tokens = sbuf("y_tokens0", T, F32)
         y2_tokens = sbuf("y_tokens2", T, F32)
-        scatter_half(y0_tokens, expert_half("bank0", "y_first0", 0, 0), expert_list, 0)
-        scatter_half(y2_tokens, expert_half("bank1", "y_first2", 2, 0), expert_list, 0)
 
-        y1_sums = psum.tile([P, T], F32, name="bank6")
-        for e in range(E):
-            product(y1_sums[:, half(e)], 1, e, w_sb, w_plane, xe_words, xe_plane)
+        def first_tile_block(b):
+            cols = slice(b * P, (b + 1) * P)
+            acc = psum.tile([P, P], F32, name=("bank0", "bank7")[b])
+            nc.tensor.matmul_mx(
+                out=acc[:],
+                lhsT=w_sb[0][:, :P].bitcast(FP8X4),
+                lhsT_scale=w_plane[:, :P],
+                rhs=xe_words[0][:, cols].bitcast(FP8X4),
+                rhs_scale=xe_plane[:, cols],
+                start=True,
+                stop=True,
+            )
+            by_slot = sbuf(f"y_block{b}", P, F32)
+            nc.vector.tensor_tensor(by_slot[:], acc[:], gate_sb[:, cols], MULT)
+            offsets = expert_list[:, b * P // LIST : (b + 1) * P // LIST]
+            nc.scalar.activation(y0_tokens[:].indirect(offsets), by_slot[:], COPY)
+
+        first_tile_block(0)
+        scatter_half(y2_tokens, expert_half("bank1", "y_first2", 2, 0), expert_list, 0)
+        first_tile_block(1)
+
         xa_planes = [gather_plane("xa_plane0", entries(adapter_list, 0))]
         xa_words = [gather_words("xa_words0", adapter_list, 0)]
-        y1_first = gated_half("y_first1", y1_sums[:, half(0)], 0)
+        y1_first = expert_half("bank6", "y_first1", 1, 0)
         xa_planes.append(gather_plane("xa_plane1", entries(adapter_list, 1)))
         xa_words.append(gather_words("xa_words1", adapter_list, 1))
         y1_tokens = sbuf("x_plane", T, F32)
         nc.vector.tensor_copy(y1_tokens[:].indirect(entries(expert_list, 0)), y1_first)
+
+        y3_sums = psum.tile([P, E, C], F32, name="bank0")
+        for e in range(E):
+            product(y3_sums[:, e, :], 3, e, w_sb, w_plane, xe_words, xe_plane)
 
         grouped = keep.tile([P, T, PACK], BF16, name="grouped", align_bytes=64)
         for b in range(T // P):
             hidden_block(b)
 
         y_second = expert_pair("bank7", "wa_placed1", [(0, 1), (2, 1)])
-        y1_second = gated_half("xa_words1", y1_sums[:, half(1)], 1)
+        y3 = keep.tile([P, E, C], F32, name="xa_words1", align_bytes=64)
+        nc.vector.tensor_tensor(y3[:], y3_sums[:], gate_sb[:].rearrange("p (e c) -> p e c", e=E), MULT)
+        y1_second_sums = psum.tile([P, C], F32, name="bank4")
+        product(y1_second_sums[:], 1, 1, w_sb, w_plane, xe_words, xe_plane)
+        y1_second = sbuf("y_second1", C, F32)
+        nc.scalar.copy(y1_second[:], y1_second_sums[:])
         scatter_half(y0_tokens, y_second[:, 0, :], expert_list, 1)
         scatter_half(y2_tokens, y_second[:, 1, :], expert_list, 1)
 
@@ -222,7 +247,9 @@ def tile_moe_mlr_relu_kernel(
         nc.vector.quantize_mx(
             out=h_words[:].bitcast(FP8X4), scales=h_plane[:], in_=grouped[:].rearrange("p m d -> p (m d)")
         )
-        nc.vector.tensor_copy(y1_tokens[:].indirect(entries(expert_list, 1)), y1_second)
+        nc.vector.tensor_tensor(
+            y1_tokens[:].indirect(entries(expert_list, 1)), y1_second[:], gate_sb[:, half(1)], MULT
+        )
         z0_sums = psum.tile([P, T], F32, name="bank2")
         for f in range(E):
             product(z0_sums[:, half(f)], 0, f, wb_sb, wb_plane, h_halves, h_plane)
@@ -230,23 +257,22 @@ def tile_moe_mlr_relu_kernel(
         nc.scalar.copy(z0[:], z0_sums[:])
         z_first = adapter_pair("bank1", "z_first", [(1, 0), (2, 0)])
         z3 = adapter_pair("bank3", "z_slots3", [(3, 0), (3, 1)])[:].rearrange("p e c -> p (e c)")
-        z_second = adapter_pair("bank4", "z_second", [(1, 1), (2, 1)])
-        y3 = expert_pair("bank1", "y_slots3", [(3, 0), (3, 1)])
+        z_second = adapter_pair("bank5", "z_second", [(1, 1), (2, 1)])
 
         z1_tokens = sbuf("z_tokens1", T, F32)
         z2_tokens = sbuf("z_tokens2", T, F32)
         for e, pair in enumerate((z_first, z_second)):
             scatter_half(z1_tokens, pair[:, 0, :], adapter_list, e)
             scatter_half(z2_tokens, pair[:, 1, :], adapter_list, e)
-        z0_tokens = sbuf("w_second", WIDE, F32)
+        z0_tokens = sbuf("wb_sb", WIDE, F32)
         nc.vector.tensor_tensor(z0_tokens[:].indirect(adapter_list[:]), z0[:], gate2_sb[:], MULT)
-        z3_tokens = sbuf("gate_sb", T, F32)
+        z3_tokens = sbuf("h_words", T, F32)
         nc.vector.tensor_copy(z3_tokens[:].indirect(adapter_list[:, : SHARE // LIST]), z3[:, :SHARE])
         nc.scalar.activation(z3_tokens[:].indirect(adapter_list[:, SHARE // LIST :]), z3[:, SHARE:], COPY)
-        y3_tokens = scatter_on_vector("y_tokens3", y3, expert_list)
+        y3_tokens = scatter_on_vector("gate2_sb", y3, expert_list)
 
         add_and_store("result0", 0, y0_tokens, z0_tokens)
-        add_and_store("w_second", 1, y1_tokens, z1_tokens)
+        add_and_store("wb_sb", 1, y1_tokens, z1_tokens)
         add_and_store("z_tokens1", 2, y2_tokens, z2_tokens)
         last = TILES - 1
         final = sbuf("z_tokens2", T, F32)

@@ -23,7 +23,7 @@ PACK = 4
 TILES = N // P
 LIST = 16
 WIDE = 768
-SHARE = 256
+SHARE = 224
 
 
 def tile_moe_mlr_relu_kernel(

@@ -20,7 +20,6 @@ ADD = mybir.AluOpType.add
 
 P = 128
 PACK = 4
-TILES = N // P
 LIST = 16
 WIDE = 768
 SHARE = 224
@@ -37,16 +36,28 @@ def tile_moe_mlr_relu_kernel(
         def sbuf(name, width, dtype):
             return keep.tile([P, width], dtype, name=name, align_bytes=64)
 
-        def load_planes(tile, scales, quadrants):
-            rows = scales.bitcast(I32)
+        def bank(number, width):
+            return psum.tile([P, width], F32, name=f"bank{number}")
+
+        def cols(first, count):
+            return slice(first, first + count)
+
+        def half(e):
+            return cols(e * C, C)
+
+        def entries(slots, span):
+            return slots[:, span.start // LIST : span.stop // LIST]
+
+        def load_rows(plane, scales, quadrants):
+            rows = scales[:, 0].bitcast(I32)
             for q in quadrants:
                 nc.sync.dma_start(
-                    out=tile[32 * q : 32 * q + 4 * E, :].bitcast(I32), in_=rows[:, 4 * q : 4 * q + 4, :]
+                    out=plane[32 * q : 32 * q + 4 * E, :].bitcast(I32), in_=rows[:, 4 * q : 4 * q + 4, :]
                 )
 
         def load_words(name, words):
-            tile = keep.tile([P, words.shape[0], words.shape[2]], I32, name=name, align_bytes=64)
-            nc.sync.dma_start(out=tile[:], in_=words.rearrange("e p n d -> p e (n d)").bitcast(I32))
+            tile = sbuf(name, T, I32)
+            nc.sync.dma_start(out=tile[:], in_=words.rearrange("p n d -> p (n d)").bitcast(I32))
             return tile
 
         def load_list(name, source):
@@ -54,16 +65,9 @@ def tile_moe_mlr_relu_kernel(
             nc.sync.dma_start(tile[:], source)
             return tile
 
-        def load_gate(name, source):
-            tile = sbuf(name, T, F32)
-            nc.sync.dma_start(out=tile[:], in_=source)
-            return tile
-
-        planes = {}
-        for name in ("w", "wa", "wb"):
-            planes[name] = sbuf(name + "_plane", T, U8)
-            nc.vector.memset(planes[name][:].bitcast(I32), 0)
-        w_plane, wa_plane, wb_plane = planes["w"], planes["wa"], planes["wb"]
+        w_plane, wa_plane, wb_plane = (sbuf(name, T, U8) for name in ("w_plane", "wa_plane", "wb_plane"))
+        for plane in (w_plane, wa_plane, wb_plane):
+            nc.vector.memset(plane[:].bitcast(I32), 0)
 
         expert_list = load_list("expert_list", offs)
         x_rows = x_scales.bitcast(I32)
@@ -73,209 +77,197 @@ def tile_moe_mlr_relu_kernel(
                 out=x_plane[32 * q : 32 * (q + 1), :T].bitcast(I32),
                 in_=x_rows[:, 4 * q : 4 * q + 4, :].broadcast_to([8, 4, T // 4]),
             )
-        x_sb = sbuf("x_sb", T, I32)
-        nc.sync.dma_start(out=x_sb[:], in_=x_words[0].rearrange("p t d -> p (t d)").bitcast(I32))
-        w_sb = [load_words("w_first", w_words[0])]
-        load_planes(w_plane, w_scales[:, 0], range(4))
+        x_sb = load_words("x_sb", x_words[0])
+        w_sb = [load_words("w_first", w_words[0, 0])]
+        load_rows(w_plane, w_scales, range(4))
+        wa_sb = [load_words("wa_first", wa_words[0, 0])]
         gate_sb = sbuf("gate_sb", T, F32)
-        nc.sync.dma_start(out=gate_sb[:, :C], in_=gate[:, :C])
-        wa_sb = [load_words("wa_first", wa_words[0])]
-        load_planes(wa_plane, wa_scales[:, 0], range(2))
+        nc.sync.dma_start(out=gate_sb[:, half(0)], in_=gate[:, half(0)])
+        load_rows(wa_plane, wa_scales, range(2))
         adapter_list = load_list("adapter_list", offs2)
-        w_sb.append(load_words("w_second", w_words[1]))
-        load_planes(wa_plane, wa_scales[:, 0], range(2, 4))
-        wa_sb.append(load_words("wa_second", wa_words[1]))
-        nc.sync.dma_start(out=gate_sb[:, C:], in_=gate[:, C:])
-        load_planes(wb_plane, wb_scales[:, 0], range(4))
-        wb_both = load_words("wb_sb", wb_words[:, 0])
+        load_rows(wa_plane, wa_scales, range(2, 4))
+        w_sb.append(load_words("w_second", w_words[1, 0]))
+        wa_sb.append(load_words("wa_second", wa_words[1, 0]))
+        nc.sync.dma_start(out=gate_sb[:, half(1)], in_=gate[:, half(1)])
+        load_rows(wb_plane, wb_scales, range(4))
+        wb_both = keep.tile([P, E, N], I32, name="wb_sb", align_bytes=64)
+        nc.sync.dma_start(out=wb_both[:], in_=wb_words[:, 0].rearrange("e p n d -> p e (n d)").bitcast(I32))
         wb_sb = [wb_both[:, f, :] for f in range(E)]
-        w_sb = [tile[:, 0, :] for tile in w_sb]
-        gate2_sb = load_gate("gate2_sb", gate2)
+        gate2_sb = sbuf("gate2_sb", T, F32)
+        nc.sync.dma_start(out=gate2_sb[:], in_=gate2)
 
-        def columns_by_place(name, source, dtype):
-            tile = keep.tile([P, PACK, P], dtype, name=name, align_bytes=64)
-            nc.gpsimd.tensor_copy(tile[:], source.rearrange("p (m t) -> p t m", t=PACK))
-            return tile
+        def by_place(source):
+            return source.rearrange("p (m t) -> p t m", t=PACK)
 
-        wa_placed = [columns_by_place("wa_placed0", wa_sb[0][:, 0, :], I32)]
-        wa_plane_placed = columns_by_place("wa_plane_placed", wa_plane[:], U8)
-        wa_placed.append(columns_by_place("wa_placed1", wa_sb[1][:, 0, :], I32))
+        wa_placed = [keep.tile([P, PACK, P], U32, name=f"wa_placed{f}", align_bytes=64) for f in range(E)]
+        wa_plane_placed = keep.tile([P, PACK, P], U8, name="wa_plane_placed", align_bytes=64)
+        nc.scalar.copy(
+            wa_placed[0][:].rearrange("p t (c i) -> p c t i", i=PACK),
+            wa_sb[0][:].bitcast(U32).rearrange("p (c i t) -> p c t i", i=PACK, t=PACK),
+        )
+        nc.gpsimd.tensor_copy(wa_plane_placed[:], by_place(wa_plane[:]))
+        nc.gpsimd.tensor_copy(wa_placed[1][:], by_place(wa_sb[1][:].bitcast(U32)))
 
-        def half(e):
-            return slice(e * C, (e + 1) * C)
+        def gather_words(into, slots, span):
+            nc.vector.tensor_copy(into[:, span], x_sb[:].bitcast(U32).indirect(entries(slots, span)))
 
-        def entries(slots, e):
-            return slots[:, e * C // LIST : (e + 1) * C // LIST]
+        def gather_bytes(into, slots, span):
+            nc.vector.tensor_copy(into[:, span], x_plane[:].indirect(entries(slots, span)))
 
-        def gather_words(name, slots, e):
-            tile = sbuf(name, C, U32)
-            nc.vector.tensor_copy(tile[:], x_sb[:].bitcast(U32).indirect(entries(slots, e)))
-            return tile[:]
-
-        def gather_plane(name, offsets):
-            tile = sbuf(name, offsets.shape[1] * LIST, U8)
-            nc.vector.tensor_copy(tile[:], x_plane[:].indirect(offsets))
-            return tile[:]
-
-        def product(acc, j, e, weights, weight_plane, words, plane):
+        def product(acc, weights, weight_plane, e, j, words, plane, span):
             nc.tensor.matmul_mx(
                 out=acc,
-                lhsT=weights[e][:, j * P : (j + 1) * P].bitcast(FP8X4),
-                lhsT_scale=weight_plane[4 * e :, j * P : (j + 1) * P],
-                rhs=words[e].bitcast(FP8X4),
-                rhs_scale=plane[:, half(e)],
+                lhsT=weights[e][:, cols(j * P, P)].bitcast(FP8X4),
+                lhsT_scale=weight_plane[4 * e :, cols(j * P, P)],
+                rhs=words[:, span].bitcast(FP8X4),
+                rhs_scale=plane[:, span],
                 start=True,
                 stop=True,
             )
 
-        def gated_pair(bank, name, pieces, weights, weight_plane, words, plane, weight):
-            acc = psum.tile([P, 2, C], F32, name=bank)
-            for place, (j, e) in enumerate(pieces):
-                product(acc[:, place, :], j, e, weights, weight_plane, words, plane)
-            e0, e1 = pieces[0][1], pieces[1][1]
-            if e0 == e1:
-                factor = weight[:, half(e0)].unsqueeze(1).broadcast_to([P, 2, C])
-            else:
-                factor = weight[:].rearrange("p (e c) -> p e c", e=E)
-            by_slot = keep.tile([P, 2, C], F32, name=name, align_bytes=64)
-            nc.vector.tensor_tensor(by_slot[:], acc[:], factor, MULT)
+        def expert_product(acc, j, span):
+            product(acc, w_sb, w_plane, span.start // C, j, xe_words, xe_plane, span)
+
+        def adapter_product(acc, j, span):
+            product(acc, wb_sb, wb_plane, span.start // C, j, h_words, h_plane, span)
+
+        def gated(name, acc, factor):
+            by_slot = keep.tile(list(acc.shape), F32, name=name, align_bytes=64)
+            nc.vector.tensor_tensor(by_slot[:], acc, factor, MULT)
             return by_slot
 
-        def scatter_half(by_token, by_slot, slots, e):
-            nc.scalar.activation(by_token[:].indirect(entries(slots, e)), by_slot, COPY)
+        def twice(factor):
+            return factor.unsqueeze(1).broadcast_to([P, 2, C])
 
-        def scatter_on_vector(name, by_slot, slots):
-            by_token = sbuf(name, WIDE, F32)
-            nc.vector.tensor_copy(by_token[:].indirect(slots[:]), by_slot[:].rearrange("p e c -> p (e c)"))
-            return by_token
+        def two_tiles(number, make, tiles, span):
+            acc = psum.tile([P, 2, C], F32, name=f"bank{number}")
+            for place, j in enumerate(tiles):
+                make(acc[:, place, :], j, span)
+            return acc
+
+        def whole_tile(number, make, j):
+            acc = bank(number, T)
+            for e in range(E):
+                make(acc[:, half(e)], j, half(e))
+            return acc
+
+        def scatter_on_scalar(by_token, slots, span, by_slot):
+            nc.scalar.activation(by_token[:].indirect(entries(slots, span)), by_slot, COPY)
+
+        def scatter_on_vector(by_token, slots, span, by_slot):
+            nc.vector.tensor_copy(by_token[:].indirect(entries(slots, span)), by_slot)
+
+        def gate_and_scatter(by_token, slots, span, by_slot, factor):
+            nc.vector.tensor_tensor(by_token[:].indirect(entries(slots, span)), by_slot, factor[:, span], MULT)
+
+        def emptied(name, acc):
+            by_slot = sbuf(name, acc.shape[1], F32)
+            nc.scalar.copy(by_slot[:], acc)
+            return by_slot
 
         def hidden_block(b):
-            f, place = divmod(b * P, C)
+            f, span = b * P // C, cols(b * P, P)
             acc = psum.tile([P, PACK, P], F32, name=f"bank{2 + b}")
             for t in range(PACK):
                 nc.tensor.matmul_mx(
                     out=acc[:, t, :],
                     lhsT=wa_placed[f][:, t, :].bitcast(FP8X4),
                     lhsT_scale=wa_plane_placed[4 * f :, t, :],
-                    rhs=xa_words[f][:, place : place + P].bitcast(FP8X4),
-                    rhs_scale=xa_planes[f][:, place : place + P],
+                    rhs=xa_words[f][:, cols(span.start - f * C, P)].bitcast(FP8X4),
+                    rhs_scale=xa_planes[f][:, cols(span.start - f * C, P)],
                     start=True,
                     stop=True,
                 )
             nc.scalar.activation(
-                grouped[:, b * P : (b + 1) * P, :].rearrange("p (c i) t -> p c t i", i=2),
+                grouped[:, span, :].rearrange("p (c i) t -> p c t i", i=2),
                 acc[:].rearrange("p t (c i) -> p c t i", i=2),
                 RELU,
             )
 
+        def gather_adapter(f):
+            plane, words = sbuf(f"xa_plane{f}", C, U8), sbuf(f"xa_words{f}", C, U32)
+            offsets = entries(adapter_list, half(f))
+            nc.vector.tensor_copy(plane[:], x_plane[:].indirect(offsets))
+            nc.vector.tensor_copy(words[:], x_sb[:].bitcast(U32).indirect(offsets))
+            xa_planes.append(plane)
+            xa_words.append(words)
+
         def add_and_store(name, j, o_tokens, z_tokens):
             result = sbuf(name, T, F32)
             nc.gpsimd.tensor_tensor(result[:], o_tokens[:, :T], z_tokens[:, :T], ADD)
-            nc.sync.dma_start(out=out[j * P : (j + 1) * P, :], in_=result[:])
+            nc.sync.dma_start(out=out[cols(j * P, P), :], in_=result[:])
 
-        def expert_pair(bank, name, pieces):
-            return gated_pair(bank, name, pieces, w_sb, w_plane, xe_words, xe_plane, gate_sb)
+        everything = cols(0, T)
+        blocks = [cols(0, P), cols(P, P)]
 
-        def adapter_pair(bank, name, pieces):
-            return gated_pair(bank, name, pieces, wb_sb, wb_plane, h_halves, h_plane, gate2_sb)
+        xe_plane, xe_words = sbuf("xe_plane", T, U8), sbuf("xe_words", T, U32)
+        gather_bytes(xe_plane, expert_list, everything)
+        for span in blocks + [half(1)]:
+            gather_words(xe_words, expert_list, span)
 
-        def gated_half(name, acc, e):
-            by_slot = sbuf(name, C, F32)
-            nc.vector.tensor_tensor(by_slot[:], acc, gate_sb[:, half(e)], MULT)
-            return by_slot[:]
+        y0_tokens, y2_tokens = sbuf("y_tokens0", T, F32), sbuf("y_tokens2", T, F32)
 
-        def expert_half(bank, name, j, e):
-            acc = psum.tile([P, C], F32, name=bank)
-            product(acc[:], j, e, w_sb, w_plane, xe_words, xe_plane)
-            return gated_half(name, acc[:], e)
+        def first_piece(number, name, j, span, by_token):
+            acc = bank(number, span.stop - span.start)
+            expert_product(acc[:], j, span)
+            scatter_on_scalar(by_token, expert_list, span, gated(name, acc[:], gate_sb[:, span])[:])
 
-        xe_plane = gather_plane("xe_plane", expert_list[:])
-        xe_words = [gather_words(f"xe_words{e}", expert_list, e) for e in range(E)]
-        y0_tokens = sbuf("y_tokens0", T, F32)
-        y2_tokens = sbuf("y_tokens2", T, F32)
+        first_piece(0, "y0_block0", 0, blocks[0], y0_tokens)
+        first_piece(1, "y2_first", 2, half(0), y2_tokens)
+        first_piece(7, "y0_block1", 0, blocks[1], y0_tokens)
 
-        def first_tile_block(b):
-            cols = slice(b * P, (b + 1) * P)
-            acc = psum.tile([P, P], F32, name=("bank0", "bank7")[b])
-            nc.tensor.matmul_mx(
-                out=acc[:],
-                lhsT=w_sb[0][:, :P].bitcast(FP8X4),
-                lhsT_scale=w_plane[:, :P],
-                rhs=xe_words[0][:, cols].bitcast(FP8X4),
-                rhs_scale=xe_plane[:, cols],
-                start=True,
-                stop=True,
-            )
-            by_slot = sbuf(f"y_block{b}", P, F32)
-            nc.vector.tensor_tensor(by_slot[:], acc[:], gate_sb[:, cols], MULT)
-            offsets = expert_list[:, b * P // LIST : (b + 1) * P // LIST]
-            nc.scalar.activation(y0_tokens[:].indirect(offsets), by_slot[:], COPY)
-
-        first_tile_block(0)
-        scatter_half(y2_tokens, expert_half("bank1", "y_first2", 2, 0), expert_list, 0)
-        first_tile_block(1)
-
-        xa_planes = [gather_plane("xa_plane0", entries(adapter_list, 0))]
-        xa_words = [gather_words("xa_words0", adapter_list, 0)]
-        y1_first = expert_half("bank6", "y_first1", 1, 0)
-        xa_planes.append(gather_plane("xa_plane1", entries(adapter_list, 1)))
-        xa_words.append(gather_words("xa_words1", adapter_list, 1))
+        xa_planes, xa_words = [], []
+        gather_adapter(0)
+        y1_first_sums = bank(6, C)
+        expert_product(y1_first_sums[:], 1, half(0))
+        y1_first = gated("y1_first", y1_first_sums[:], gate_sb[:, half(0)])
+        gather_adapter(1)
         y1_tokens = sbuf("x_plane", T, F32)
-        nc.vector.tensor_copy(y1_tokens[:].indirect(entries(expert_list, 0)), y1_first)
+        scatter_on_vector(y1_tokens, expert_list, half(0), y1_first[:])
 
-        y3_sums = psum.tile([P, E, C], F32, name="bank0")
-        for e in range(E):
-            product(y3_sums[:, e, :], 3, e, w_sb, w_plane, xe_words, xe_plane)
+        y3_sums = whole_tile(0, expert_product, 3)
+        y_second_sums = two_tiles(7, expert_product, (0, 2), half(1))
 
         grouped = keep.tile([P, T, PACK], BF16, name="grouped", align_bytes=64)
         for b in range(T // P):
             hidden_block(b)
 
-        y_second = expert_pair("bank7", "wa_placed1", [(0, 1), (2, 1)])
-        y3 = keep.tile([P, E, C], F32, name="xa_words1", align_bytes=64)
-        nc.vector.tensor_tensor(y3[:], y3_sums[:], gate_sb[:].rearrange("p (e c) -> p e c", e=E), MULT)
-        y1_second_sums = psum.tile([P, C], F32, name="bank4")
-        product(y1_second_sums[:], 1, 1, w_sb, w_plane, xe_words, xe_plane)
-        y1_second = sbuf("y_second1", C, F32)
-        nc.scalar.copy(y1_second[:], y1_second_sums[:])
-        scatter_half(y0_tokens, y_second[:, 0, :], expert_list, 1)
-        scatter_half(y2_tokens, y_second[:, 1, :], expert_list, 1)
+        y_second = gated("wa_placed1", y_second_sums[:], twice(gate_sb[:, half(1)]))
+        y3 = gated("xa_words1", y3_sums[:], gate_sb[:])
+        y1_second_sums = bank(3, C)
+        expert_product(y1_second_sums[:], 1, half(1))
+        y1_second = gated("y1_second", y1_second_sums[:], gate_sb[:, half(1)])
+        scatter_on_scalar(y0_tokens, expert_list, half(1), y_second[:, 0, :])
+        scatter_on_scalar(y2_tokens, expert_list, half(1), y_second[:, 1, :])
 
-        h_words = sbuf("h_words", T, U32)
-        h_plane = sbuf("h_plane", T, U8)
-        h_halves = [h_words[:, half(e)] for e in range(E)]
+        h_words, h_plane = sbuf("h_words", T, U32), sbuf("h_plane", T, U8)
         nc.vector.quantize_mx(
             out=h_words[:].bitcast(FP8X4), scales=h_plane[:], in_=grouped[:].rearrange("p m d -> p (m d)")
         )
-        nc.vector.tensor_tensor(
-            y1_tokens[:].indirect(entries(expert_list, 1)), y1_second[:], gate_sb[:, half(1)], MULT
-        )
-        z0_sums = psum.tile([P, T], F32, name="bank2")
-        for f in range(E):
-            product(z0_sums[:, half(f)], 0, f, wb_sb, wb_plane, h_halves, h_plane)
-        z0 = sbuf("z_slots0", T, F32)
-        nc.scalar.copy(z0[:], z0_sums[:])
-        z_first = adapter_pair("bank1", "z_first", [(1, 0), (2, 0)])
-        z3 = adapter_pair("bank3", "z_slots3", [(3, 0), (3, 1)])[:].rearrange("p e c -> p (e c)")
-        z_second = adapter_pair("bank5", "z_second", [(1, 1), (2, 1)])
+        scatter_on_vector(y1_tokens, expert_list, half(1), y1_second[:])
 
-        z1_tokens = sbuf("z_tokens1", T, F32)
-        z2_tokens = sbuf("z_tokens2", T, F32)
+        z_first = gated("z_first", two_tiles(1, adapter_product, (1, 2), half(0))[:], twice(gate2_sb[:, half(0)]))
+        z0 = emptied("z0_slots", whole_tile(2, adapter_product, 0)[:])
+        z3 = gated("z3_slots", whole_tile(4, adapter_product, 3)[:], gate2_sb[:])
+        z_second = gated("z_second", two_tiles(5, adapter_product, (1, 2), half(1))[:], twice(gate2_sb[:, half(1)]))
+
+        z1_tokens, z2_tokens = sbuf("z_tokens1", T, F32), sbuf("z_tokens2", T, F32)
         for e, pair in enumerate((z_first, z_second)):
-            scatter_half(z1_tokens, pair[:, 0, :], adapter_list, e)
-            scatter_half(z2_tokens, pair[:, 1, :], adapter_list, e)
+            scatter_on_scalar(z1_tokens, adapter_list, half(e), pair[:, 0, :])
+            scatter_on_scalar(z2_tokens, adapter_list, half(e), pair[:, 1, :])
         z0_tokens = sbuf("wb_sb", WIDE, F32)
-        nc.vector.tensor_tensor(z0_tokens[:].indirect(adapter_list[:]), z0[:], gate2_sb[:], MULT)
+        gate_and_scatter(z0_tokens, adapter_list, everything, z0[:], gate2_sb)
         z3_tokens = sbuf("h_words", T, F32)
-        nc.vector.tensor_copy(z3_tokens[:].indirect(adapter_list[:, : SHARE // LIST]), z3[:, :SHARE])
-        nc.scalar.activation(z3_tokens[:].indirect(adapter_list[:, SHARE // LIST :]), z3[:, SHARE:], COPY)
-        y3_tokens = scatter_on_vector("gate2_sb", y3, expert_list)
+        mine, rest = cols(0, SHARE), cols(SHARE, T - SHARE)
+        scatter_on_vector(z3_tokens, adapter_list, mine, z3[:, mine])
+        scatter_on_scalar(z3_tokens, adapter_list, rest, z3[:, rest])
+        y3_tokens = sbuf("gate2_sb", WIDE, F32)
+        scatter_on_vector(y3_tokens, expert_list, everything, y3[:])
 
         add_and_store("result0", 0, y0_tokens, z0_tokens)
         add_and_store("wb_sb", 1, y1_tokens, z1_tokens)
         add_and_store("z_tokens1", 2, y2_tokens, z2_tokens)
-        last = TILES - 1
         final = sbuf("z_tokens2", T, F32)
         for e in range(2):
             nc.vector.tensor_tensor(final[:, half(e)], y3_tokens[:, half(e)], z3_tokens[:, half(e)], ADD)
-            nc.sync.dma_start(out=out[last * P :, half(e)], in_=final[:, half(e)])
+            nc.sync.dma_start(out=out[cols(3 * P, P), half(e)], in_=final[:, half(e)])

@@ -80,13 +80,12 @@ def tile_moe_mlr_relu_kernel(
         x_sb = load_words("x_sb", x_words[0])
         w_sb = [load_words("w_first", w_words[0, 0])]
         load_rows(w_plane, w_scales, range(4))
-        wa_sb = [load_words("wa_first", wa_words[0, 0])]
         gate_sb = sbuf("gate_sb", T, F32)
         nc.sync.dma_start(out=gate_sb[:, half(0)], in_=gate[:, half(0)])
-        load_rows(wa_plane, wa_scales, range(2))
+        wa_sb = [load_words("wa_first", wa_words[0, 0])]
         adapter_list = load_list("adapter_list", offs2)
-        load_rows(wa_plane, wa_scales, range(2, 4))
         w_sb.append(load_words("w_second", w_words[1, 0]))
+        load_rows(wa_plane, wa_scales, range(4))
         wa_sb.append(load_words("wa_second", wa_words[1, 0]))
         nc.sync.dma_start(out=gate_sb[:, half(1)], in_=gate[:, half(1)])
         load_rows(wb_plane, wb_scales, range(4))
@@ -101,10 +100,7 @@ def tile_moe_mlr_relu_kernel(
 
         wa_placed = [keep.tile([P, PACK, P], U32, name=f"wa_placed{f}", align_bytes=64) for f in range(E)]
         wa_plane_placed = keep.tile([P, PACK, P], U8, name="wa_plane_placed", align_bytes=64)
-        nc.scalar.copy(
-            wa_placed[0][:].rearrange("p t (c i) -> p c t i", i=PACK),
-            wa_sb[0][:].bitcast(U32).rearrange("p (c i t) -> p c t i", i=PACK, t=PACK),
-        )
+        nc.gpsimd.tensor_copy(wa_placed[0][:], by_place(wa_sb[0][:].bitcast(U32)))
         nc.gpsimd.tensor_copy(wa_plane_placed[:], by_place(wa_plane[:]))
         nc.gpsimd.tensor_copy(wa_placed[1][:], by_place(wa_sb[1][:].bitcast(U32)))
 

@@ -22,7 +22,8 @@ P = 128
 PACK = 4
 LIST = 16
 WIDE = 768
-SHARE = 224
+EARLY = 192
+LATE = 192
 
 
 def tile_moe_mlr_relu_kernel(
@@ -33,11 +34,11 @@ def tile_moe_mlr_relu_kernel(
         keep = ctx.enter_context(tc.tile_pool(name="keep", bufs=1))
         psum = ctx.enter_context(tc.psum_pool(name="psum", bufs=1))
 
-        def sbuf(name, width, dtype):
-            return keep.tile([P, width], dtype, name=name, align_bytes=64)
+        def sbuf(name, shape, dtype):
+            return keep.tile([P, *shape], dtype, name=name, align_bytes=64)
 
-        def bank(number, width):
-            return psum.tile([P, width], F32, name=f"bank{number}")
+        def bank(number, shape):
+            return psum.tile([P, *shape], F32, name=f"bank{number}")
 
         def cols(first, count):
             return slice(first, first + count)
@@ -48,15 +49,15 @@ def tile_moe_mlr_relu_kernel(
         def entries(slots, span):
             return slots[:, span.start // LIST : span.stop // LIST]
 
-        def load_rows(plane, scales, quadrants):
+        def load_rows(plane, scales):
             rows = scales[:, 0].bitcast(I32)
-            for q in quadrants:
+            for q in range(4):
                 nc.sync.dma_start(
                     out=plane[32 * q : 32 * q + 4 * E, :].bitcast(I32), in_=rows[:, 4 * q : 4 * q + 4, :]
                 )
 
         def load_words(name, words):
-            tile = sbuf(name, T, I32)
+            tile = sbuf(name, [T], I32)
             nc.sync.dma_start(out=tile[:], in_=words.rearrange("p n d -> p (n d)").bitcast(I32))
             return tile
 
@@ -65,13 +66,13 @@ def tile_moe_mlr_relu_kernel(
             nc.sync.dma_start(tile[:], source)
             return tile
 
-        w_plane, wa_plane, wb_plane = (sbuf(name, T, U8) for name in ("w_plane", "wa_plane", "wb_plane"))
+        w_plane, wa_plane, wb_plane = (sbuf(name, [T], U8) for name in ("w_plane", "wa_plane", "wb_plane"))
         for plane in (w_plane, wa_plane, wb_plane):
             nc.vector.memset(plane[:].bitcast(I32), 0)
 
         expert_list = load_list("expert_list", offs)
         x_rows = x_scales.bitcast(I32)
-        x_plane = sbuf("x_plane", WIDE, U8)
+        x_plane = sbuf("x_plane", [WIDE], U8)
         for q, queue in enumerate((nc.scalar, nc.scalar, nc.sync, nc.sync)):
             queue.dma_start(
                 out=x_plane[32 * q : 32 * (q + 1), :T].bitcast(I32),
@@ -79,72 +80,58 @@ def tile_moe_mlr_relu_kernel(
             )
         x_sb = load_words("x_sb", x_words[0])
         w_sb = [load_words("w_first", w_words[0, 0])]
-        load_rows(w_plane, w_scales, range(4))
-        gate_sb = sbuf("gate_sb", T, F32)
+        load_rows(w_plane, w_scales)
+        gate_sb = sbuf("gate_sb", [T], F32)
         nc.sync.dma_start(out=gate_sb[:, half(0)], in_=gate[:, half(0)])
         wa_sb = [load_words("wa_first", wa_words[0, 0])]
         adapter_list = load_list("adapter_list", offs2)
-        w_sb.append(load_words("w_second", w_words[1, 0]))
-        load_rows(wa_plane, wa_scales, range(4))
-        wa_sb.append(load_words("wa_second", wa_words[1, 0]))
         nc.sync.dma_start(out=gate_sb[:, half(1)], in_=gate[:, half(1)])
-        load_rows(wb_plane, wb_scales, range(4))
-        wb_both = keep.tile([P, E, N], I32, name="wb_sb", align_bytes=64)
+        w_sb.append(load_words("w_second", w_words[1, 0]))
+        load_rows(wa_plane, wa_scales)
+        wa_sb.append(load_words("wa_second", wa_words[1, 0]))
+        load_rows(wb_plane, wb_scales)
+        wb_both = sbuf("wb_sb", [E, N], I32)
         nc.sync.dma_start(out=wb_both[:], in_=wb_words[:, 0].rearrange("e p n d -> p e (n d)").bitcast(I32))
-        wb_sb = [wb_both[:, f, :] for f in range(E)]
-        gate2_sb = sbuf("gate2_sb", T, F32)
+        gate2_sb = sbuf("gate2_sb", [T], F32)
         nc.sync.dma_start(out=gate2_sb[:], in_=gate2)
 
         def by_place(source):
             return source.rearrange("p (m t) -> p t m", t=PACK)
 
-        wa_placed = [keep.tile([P, PACK, P], U32, name=f"wa_placed{f}", align_bytes=64) for f in range(E)]
-        wa_plane_placed = keep.tile([P, PACK, P], U8, name="wa_plane_placed", align_bytes=64)
+        wa_placed = [sbuf(f"wa_placed{f}", [PACK, P], U32) for f in range(E)]
+        wa_plane_placed = sbuf("wa_plane_placed", [PACK, P], U8)
         nc.gpsimd.tensor_copy(wa_placed[0][:], by_place(wa_sb[0][:].bitcast(U32)))
         nc.gpsimd.tensor_copy(wa_plane_placed[:], by_place(wa_plane[:]))
         nc.gpsimd.tensor_copy(wa_placed[1][:], by_place(wa_sb[1][:].bitcast(U32)))
 
-        def gather_words(into, slots, span):
-            nc.vector.tensor_copy(into[:, span], x_sb[:].bitcast(U32).indirect(entries(slots, span)))
-
-        def gather_bytes(into, slots, span):
-            nc.vector.tensor_copy(into[:, span], x_plane[:].indirect(entries(slots, span)))
-
-        def product(acc, weights, weight_plane, e, j, words, plane, span):
+        def product(acc, weights, weight_plane, words, plane):
             nc.tensor.matmul_mx(
                 out=acc,
-                lhsT=weights[e][:, cols(j * P, P)].bitcast(FP8X4),
-                lhsT_scale=weight_plane[4 * e :, cols(j * P, P)],
-                rhs=words[:, span].bitcast(FP8X4),
-                rhs_scale=plane[:, span],
+                lhsT=weights.bitcast(FP8X4),
+                lhsT_scale=weight_plane,
+                rhs=words.bitcast(FP8X4),
+                rhs_scale=plane,
                 start=True,
                 stop=True,
             )
 
         def expert_product(acc, j, span):
-            product(acc, w_sb, w_plane, span.start // C, j, xe_words, xe_plane, span)
+            e = span.start // C
+            product(acc, w_sb[e][:, cols(j * P, P)], w_plane[4 * e :, cols(j * P, P)], xe_words[:, span], xe_plane[:, span])
 
-        def adapter_product(acc, j, span):
-            product(acc, wb_sb, wb_plane, span.start // C, j, h_words, h_plane, span)
+        def adapter_product(acc, j, f):
+            product(acc, wb_both[:, f, cols(j * P, P)], wb_plane[4 * f :, cols(j * P, P)], h_words[f][:], h_planes[f][:])
 
-        def gated(name, acc, factor):
-            by_slot = keep.tile(list(acc.shape), F32, name=name, align_bytes=64)
-            nc.vector.tensor_tensor(by_slot[:], acc, factor, MULT)
-            return by_slot
+        def gate_into(by_slot, acc, factor):
+            nc.vector.tensor_tensor(by_slot, acc, factor, MULT)
 
         def twice(factor):
             return factor.unsqueeze(1).broadcast_to([P, 2, C])
 
-        def two_tiles(number, make, tiles, span):
-            acc = psum.tile([P, 2, C], F32, name=f"bank{number}")
+        def two_tiles(number, make, tiles, where):
+            acc = bank(number, [2, C])
             for place, j in enumerate(tiles):
-                make(acc[:, place, :], j, span)
-            return acc
-
-        def whole_tile(number, make, j):
-            acc = bank(number, T)
-            for e in range(E):
-                make(acc[:, half(e)], j, half(e))
+                make(acc[:, place, :], j, where)
             return acc
 
         def scatter_on_scalar(by_token, slots, span, by_slot):
@@ -153,117 +140,130 @@ def tile_moe_mlr_relu_kernel(
         def scatter_on_vector(by_token, slots, span, by_slot):
             nc.vector.tensor_copy(by_token[:].indirect(entries(slots, span)), by_slot)
 
-        def gate_and_scatter(by_token, slots, span, by_slot, factor):
-            nc.vector.tensor_tensor(by_token[:].indirect(entries(slots, span)), by_slot, factor[:, span], MULT)
-
-        def emptied(name, acc):
-            by_slot = sbuf(name, acc.shape[1], F32)
-            nc.scalar.copy(by_slot[:], acc)
-            return by_slot
-
         def hidden_block(b):
-            f, span = b * P // C, cols(b * P, P)
-            acc = psum.tile([P, PACK, P], F32, name=f"bank{2 + b}")
+            f, span = b * P // C, cols(b * P % C, P)
+            acc = bank(2 + b, [PACK, P])
             for t in range(PACK):
-                nc.tensor.matmul_mx(
-                    out=acc[:, t, :],
-                    lhsT=wa_placed[f][:, t, :].bitcast(FP8X4),
-                    lhsT_scale=wa_plane_placed[4 * f :, t, :],
-                    rhs=xa_words[f][:, cols(span.start - f * C, P)].bitcast(FP8X4),
-                    rhs_scale=xa_planes[f][:, cols(span.start - f * C, P)],
-                    start=True,
-                    stop=True,
+                product(
+                    acc[:, t, :], wa_placed[f][:, t, :], wa_plane_placed[4 * f :, t, :],
+                    xa_words[f][:, span], xa_planes[f][:, span],
                 )
             nc.scalar.activation(
-                grouped[:, span, :].rearrange("p (c i) t -> p c t i", i=2),
+                grouped[f][:, span, :].rearrange("p (c i) t -> p c t i", i=2),
                 acc[:].rearrange("p t (c i) -> p c t i", i=2),
                 RELU,
             )
 
-        def gather_adapter(f):
-            plane, words = sbuf(f"xa_plane{f}", C, U8), sbuf(f"xa_words{f}", C, U32)
-            offsets = entries(adapter_list, half(f))
-            nc.vector.tensor_copy(plane[:], x_plane[:].indirect(offsets))
-            nc.vector.tensor_copy(words[:], x_sb[:].bitcast(U32).indirect(offsets))
+        def gather_adapter_bytes(name, f):
+            plane = sbuf(name, [C], U8)
+            nc.vector.tensor_copy(plane[:], x_plane[:].indirect(entries(adapter_list, half(f))))
             xa_planes.append(plane)
+
+        def gather_adapter_words(name, f):
+            words = sbuf(name, [C], U32)
+            nc.vector.tensor_copy(words[:], x_sb[:].bitcast(U32).indirect(entries(adapter_list, half(f))))
             xa_words.append(words)
 
+        def quantise(f):
+            words, plane = sbuf(f"h_words{f}", [C], U32), sbuf(f"h_plane{f}", [C], U8)
+            nc.vector.quantize_mx(
+                out=words[:].bitcast(FP8X4), scales=plane[:], in_=grouped[f][:].rearrange("p m d -> p (m d)")
+            )
+            h_words.append(words)
+            h_planes.append(plane)
+
         def add_and_store(name, j, o_tokens, z_tokens):
-            result = sbuf(name, T, F32)
+            result = sbuf(name, [T], F32)
             nc.gpsimd.tensor_tensor(result[:], o_tokens[:, :T], z_tokens[:, :T], ADD)
             nc.sync.dma_start(out=out[cols(j * P, P), :], in_=result[:])
 
         everything = cols(0, T)
         blocks = [cols(0, P), cols(P, P)]
 
-        xe_plane, xe_words = sbuf("xe_plane", T, U8), sbuf("xe_words", T, U32)
-        gather_bytes(xe_plane, expert_list, everything)
+        xe_plane, xe_words = sbuf("xe_plane", [T], U8), sbuf("xe_words", [T], U32)
+        nc.vector.tensor_copy(xe_plane[:], x_plane[:].indirect(expert_list[:]))
         for span in blocks + [half(1)]:
-            gather_words(xe_words, expert_list, span)
+            nc.vector.tensor_copy(xe_words[:, span], x_sb[:].bitcast(U32).indirect(entries(expert_list, span)))
 
-        y0_tokens, y2_tokens = sbuf("y_tokens0", T, F32), sbuf("y_tokens2", T, F32)
+        y0_tokens, y1_tokens, y2_tokens = (sbuf(f"y_tokens{j}", [T], F32) for j in range(3))
 
-        def first_piece(number, name, j, span, by_token):
-            acc = bank(number, span.stop - span.start)
-            expert_product(acc[:], j, span)
-            scatter_on_scalar(by_token, expert_list, span, gated(name, acc[:], gate_sb[:, span])[:])
+        def first_block(number, b):
+            acc = bank(number, [P])
+            expert_product(acc[:], 0, blocks[b])
+            by_slot = sbuf(f"y0_block{b}", [P], F32)
+            gate_into(by_slot[:], acc[:], gate_sb[:, blocks[b]])
+            scatter_on_scalar(y0_tokens, expert_list, blocks[b], by_slot[:])
 
-        first_piece(0, "y0_block0", 0, blocks[0], y0_tokens)
-        first_piece(1, "y2_first", 2, half(0), y2_tokens)
-        first_piece(7, "y0_block1", 0, blocks[1], y0_tokens)
+        first_block(0, 0)
+        y21 = sbuf("y21_slots", [3, C], F32)
+        y1_slots = y21[:, 1:3, :].rearrange("p e c -> p (e c)")
+        for number, j, place in ((1, 1, 1), (6, 2, 0)):
+            acc = bank(number, [C])
+            expert_product(acc[:], j, half(0))
+            gate_into(y21[:, place, :], acc[:], gate_sb[:, half(0)])
+        early, rest = cols(0, EARLY), cols(EARLY, T - EARLY)
+        scatter_on_scalar(y1_tokens, expert_list, early, y1_slots[:, early])
+        scatter_on_scalar(y2_tokens, expert_list, half(0), y21[:, 0, :])
+        first_block(7, 1)
 
         xa_planes, xa_words = [], []
-        gather_adapter(0)
-        y1_first_sums = bank(6, C)
-        expert_product(y1_first_sums[:], 1, half(0))
-        y1_first = gated("y1_first", y1_first_sums[:], gate_sb[:, half(0)])
-        gather_adapter(1)
-        y1_tokens = sbuf("x_plane", T, F32)
-        scatter_on_vector(y1_tokens, expert_list, half(0), y1_first[:])
+        gather_adapter_bytes("xa_plane0", 0)
+        gather_adapter_words("xa_words0", 0)
+        gather_adapter_bytes("xa_plane1", 1)
 
-        y3_sums = whole_tile(0, expert_product, 3)
+        y3_sums = bank(0, [T])
+        expert_product(y3_sums[:, half(0)], 3, half(0))
+        y1_second_sums = bank(5, [C])
+        expert_product(y1_second_sums[:], 1, half(1))
+        gate_into(y21[:, 2, :], y1_second_sums[:], gate_sb[:, half(1)])
+        expert_product(y3_sums[:, half(1)], 3, half(1))
         y_second_sums = two_tiles(7, expert_product, (0, 2), half(1))
 
-        grouped = keep.tile([P, T, PACK], BF16, name="grouped", align_bytes=64)
+        gather_adapter_words("w_second", 1)
+        scatter_on_vector(y1_tokens, expert_list, rest, y1_slots[:, rest])
+
+        grouped = [sbuf(f"grouped{f}", [C, PACK], BF16) for f in range(E)]
         for b in range(T // P):
             hidden_block(b)
 
-        y_second = gated("wa_placed1", y_second_sums[:], twice(gate_sb[:, half(1)]))
-        y3 = gated("xa_words1", y3_sums[:], gate_sb[:])
-        y1_second_sums = bank(3, C)
-        expert_product(y1_second_sums[:], 1, half(1))
-        y1_second = gated("y1_second", y1_second_sums[:], gate_sb[:, half(1)])
+        h_words, h_planes = [], []
+        y_second = sbuf("wa_placed1", [2, C], F32)
+        gate_into(y_second[:], y_second_sums[:], twice(gate_sb[:, half(1)]))
+        quantise(0)
+        y3_slots = sbuf("w_second", [T], F32)
+        gate_into(y3_slots[:], y3_sums[:], gate_sb[:])
+        scatter_on_vector(y2_tokens, expert_list, cols(C + P, P), y_second[:, 1, blocks[1]])
+        quantise(1)
         scatter_on_scalar(y0_tokens, expert_list, half(1), y_second[:, 0, :])
-        scatter_on_scalar(y2_tokens, expert_list, half(1), y_second[:, 1, :])
+        scatter_on_scalar(y2_tokens, expert_list, cols(C, P), y_second[:, 1, blocks[0]])
 
-        h_words, h_plane = sbuf("h_words", T, U32), sbuf("h_plane", T, U8)
-        nc.vector.quantize_mx(
-            out=h_words[:].bitcast(FP8X4), scales=h_plane[:], in_=grouped[:].rearrange("p m d -> p (m d)")
-        )
-        scatter_on_vector(y1_tokens, expert_list, half(1), y1_second[:])
+        z12 = [sbuf(f"z12_slots{f}", [2, C], F32) for f in range(E)]
+        z03 = sbuf("z03_slots", [2, T], F32)
+        for number, by_slot, tiles, f in (
+            (1, z12[0][:], (1, 2), 0),
+            (6, z03[:, :, half(0)], (0, 3), 0),
+            (2, z03[:, :, half(1)], (0, 3), 1),
+            (3, z12[1][:], (1, 2), 1),
+        ):
+            gate_into(by_slot, two_tiles(number, adapter_product, tiles, f)[:], twice(gate2_sb[:, half(f)]))
 
-        z_first = gated("z_first", two_tiles(1, adapter_product, (1, 2), half(0))[:], twice(gate2_sb[:, half(0)]))
-        z0 = emptied("z0_slots", whole_tile(2, adapter_product, 0)[:])
-        z3 = gated("z3_slots", whole_tile(4, adapter_product, 3)[:], gate2_sb[:])
-        z_second = gated("z_second", two_tiles(5, adapter_product, (1, 2), half(1))[:], twice(gate2_sb[:, half(1)]))
-
-        z1_tokens, z2_tokens = sbuf("z_tokens1", T, F32), sbuf("z_tokens2", T, F32)
-        for e, pair in enumerate((z_first, z_second)):
-            scatter_on_scalar(z1_tokens, adapter_list, half(e), pair[:, 0, :])
-            scatter_on_scalar(z2_tokens, adapter_list, half(e), pair[:, 1, :])
-        z0_tokens = sbuf("wb_sb", WIDE, F32)
-        gate_and_scatter(z0_tokens, adapter_list, everything, z0[:], gate2_sb)
-        z3_tokens = sbuf("h_words", T, F32)
-        mine, rest = cols(0, SHARE), cols(SHARE, T - SHARE)
-        scatter_on_vector(z3_tokens, adapter_list, mine, z3[:, mine])
-        scatter_on_scalar(z3_tokens, adapter_list, rest, z3[:, rest])
-        y3_tokens = sbuf("gate2_sb", WIDE, F32)
-        scatter_on_vector(y3_tokens, expert_list, everything, y3[:])
+        z1_tokens, z2_tokens = sbuf("z_tokens1", [T], F32), sbuf("z_tokens2", [T], F32)
+        for f in range(E):
+            scatter_on_scalar(z1_tokens, adapter_list, half(f), z12[f][:, 0, :])
+            scatter_on_scalar(z2_tokens, adapter_list, half(f), z12[f][:, 1, :])
+        z0_tokens = sbuf("wb_sb", [WIDE], F32)
+        scatter_on_vector(z0_tokens, adapter_list, everything, z03[:, 0, :])
+        z3_tokens = sbuf("h_words1", [T], F32)
+        mine, others = cols(0, LATE), cols(LATE, T - LATE)
+        scatter_on_vector(z3_tokens, adapter_list, mine, z03[:, 1, mine])
+        scatter_on_scalar(z3_tokens, adapter_list, others, z03[:, 1, others])
+        y3_tokens = sbuf("gate2_sb", [WIDE], F32)
+        scatter_on_vector(y3_tokens, expert_list, everything, y3_slots[:])
 
         add_and_store("result0", 0, y0_tokens, z0_tokens)
         add_and_store("wb_sb", 1, y1_tokens, z1_tokens)
         add_and_store("z_tokens1", 2, y2_tokens, z2_tokens)
-        final = sbuf("z_tokens2", T, F32)
+        final = sbuf("z_tokens2", [T], F32)
         for e in range(2):
             nc.vector.tensor_tensor(final[:, half(e)], y3_tokens[:, half(e)], z3_tokens[:, half(e)], ADD)
             nc.sync.dma_start(out=out[cols(3 * P, P), half(e)], in_=final[:, half(e)])

@@ -146,18 +146,13 @@ def tile_moe_mlr_relu_kernel(
             for t in range(PACK):
                 product(
                     acc[:, t, :], wa_placed[f][:, t, :], wa_plane_placed[4 * f :, t, :],
-                    xa_words[f][:, span], xa_planes[f][:, span],
+                    xa_words[f][:, span], xa_plane[:, cols(b * P, P)],
                 )
             nc.scalar.activation(
                 grouped[f][:, span, :].rearrange("p (c i) t -> p c t i", i=2),
                 acc[:].rearrange("p t (c i) -> p c t i", i=2),
                 RELU,
             )
-
-        def gather_adapter_bytes(name, f):
-            plane = sbuf(name, [C], U8)
-            nc.vector.tensor_copy(plane[:], x_plane[:].indirect(entries(adapter_list, half(f))))
-            xa_planes.append(plane)
 
         def gather_adapter_words(name, f):
             words = sbuf(name, [C], U32)
@@ -206,10 +201,9 @@ def tile_moe_mlr_relu_kernel(
         scatter_on_scalar(y2_tokens, expert_list, half(0), y21[:, 0, :])
         first_block(7, 1)
 
-        xa_planes, xa_words = [], []
-        gather_adapter_bytes("xa_plane0", 0)
+        xa_plane, xa_words = sbuf("xa_plane", [T], U8), []
+        nc.vector.tensor_copy(xa_plane[:], x_plane[:].indirect(adapter_list[:]))
         gather_adapter_words("xa_words0", 0)
-        gather_adapter_bytes("xa_plane1", 1)
 
         y3_sums = bank(0, [T])
         expert_product(y3_sums[:, half(0)], 3, half(0))

@@ -231,20 +231,20 @@ def tile_moe_mlr_relu_kernel(
         scatter_on_scalar(y0_tokens, expert_list, half(1), y_second[:, 0, :])
         scatter_on_scalar(y2_tokens, expert_list, cols(C, P), y_second[:, 1, blocks[0]])
 
-        z12 = [sbuf(f"z12_slots{f}", [2, C], F32) for f in range(E)]
+        z12 = sbuf("z12_slots", [2, T], F32)
         z03 = sbuf("z03_slots", [2, T], F32)
         for number, by_slot, tiles, f in (
-            (1, z12[0][:], (1, 2), 0),
+            (1, z12[:, :, half(0)], (1, 2), 0),
             (6, z03[:, :, half(0)], (0, 3), 0),
             (2, z03[:, :, half(1)], (0, 3), 1),
-            (3, z12[1][:], (1, 2), 1),
+            (3, z12[:, :, half(1)], (1, 2), 1),
         ):
             gate_into(by_slot, two_tiles(number, adapter_product, tiles, f)[:], twice(gate2_sb[:, half(f)]))
 
         z1_tokens, z2_tokens = sbuf("z_tokens1", [T], F32), sbuf("z_tokens2", [T], F32)
-        for f in range(E):
-            scatter_on_scalar(z1_tokens, adapter_list, half(f), z12[f][:, 0, :])
-            scatter_on_scalar(z2_tokens, adapter_list, half(f), z12[f][:, 1, :])
+        for one, two in ((half(0), blocks[0]), (half(1), cols(P, T - P))):
+            scatter_on_scalar(z1_tokens, adapter_list, one, z12[:, 0, one])
+            scatter_on_scalar(z2_tokens, adapter_list, two, z12[:, 1, two])
         z0_tokens = sbuf("wb_sb", [WIDE], F32)
         scatter_on_vector(z0_tokens, adapter_list, everything, z03[:, 0, :])
         z3_tokens = sbuf("h_words1", [T], F32)
@@ -254,9 +254,9 @@ def tile_moe_mlr_relu_kernel(
         y3_tokens = sbuf("gate2_sb", [WIDE], F32)
         scatter_on_vector(y3_tokens, expert_list, everything, y3_slots[:])
 
-        add_and_store("result0", 0, y0_tokens, z0_tokens)
-        add_and_store("wb_sb", 1, y1_tokens, z1_tokens)
-        add_and_store("z_tokens1", 2, y2_tokens, z2_tokens)
+        add_and_store("result1", 1, y1_tokens, z1_tokens)
+        add_and_store("z_tokens1", 0, y0_tokens, z0_tokens)
+        add_and_store("wb_sb", 2, y2_tokens, z2_tokens)
         final = sbuf("z_tokens2", [T], F32)
         for e in range(2):
             nc.vector.tensor_tensor(final[:, half(e)], y3_tokens[:, half(e)], z3_tokens[:, half(e)], ADD)

from contextlib import ExitStack

import concourse.mybir as mybir

K, T, N, H = 512, 512, 512, 512
E, C = 2, 256
FLOPS = 2 * (K * N + K * H + H * N) * T

F32 = mybir.dt.float32
BF16 = mybir.dt.bfloat16
I32 = mybir.dt.int32
U32 = mybir.dt.uint32
U16 = mybir.dt.uint16
U8 = mybir.dt.uint8
FP8X4 = mybir.dt.float8_e4m3fn_x4
RELU = mybir.ActivationFunctionType.Relu
COPY = mybir.ActivationFunctionType.Copy
MULT = mybir.AluOpType.mult
ADD = mybir.AluOpType.add

P = 128
PACK = 4
LIST = 16
WIDE = 768
EARLY = 192
LATE = 192


def tile_moe_mlr_relu_kernel(
    tc, x_words, x_scales, w_words, w_scales, wa_words, wa_scales, wb_words, wb_scales, gate, gate2, offs, offs2, out
):
    nc = tc.nc
    with ExitStack() as ctx:
        keep = ctx.enter_context(tc.tile_pool(name="keep", bufs=1))
        psum = ctx.enter_context(tc.psum_pool(name="psum", bufs=1))

        def sbuf(name, shape, dtype):
            return keep.tile([P, *shape], dtype, name=name, align_bytes=64)

        def bank(number, shape):
            return psum.tile([P, *shape], F32, name=f"bank{number}")

        def cols(first, count):
            return slice(first, first + count)

        def half(e):
            return cols(e * C, C)

        def entries(slots, span):
            return slots[:, span.start // LIST : span.stop // LIST]

        def load_rows(plane, scales):
            rows = scales[:, 0].bitcast(I32)
            for q in range(4):
                nc.sync.dma_start(
                    out=plane[32 * q : 32 * q + 4 * E, :].bitcast(I32), in_=rows[:, 4 * q : 4 * q + 4, :]
                )

        def load_words(name, words):
            tile = sbuf(name, [T], I32)
            nc.sync.dma_start(out=tile[:], in_=words.rearrange("p n d -> p (n d)").bitcast(I32))
            return tile

        def load_list(name, source):
            tile = keep.tile([P, T // LIST], U16, name=name)
            nc.sync.dma_start(tile[:], source)
            return tile

        w_plane, wa_plane, wb_plane = (sbuf(name, [T], U8) for name in ("w_plane", "wa_plane", "wb_plane"))
        for plane in (w_plane, wa_plane, wb_plane):
            nc.vector.memset(plane[:].bitcast(I32), 0)

        expert_list = load_list("expert_list", offs)
        x_rows = x_scales.bitcast(I32)
        x_plane = sbuf("x_plane", [WIDE], U8)
        for q, queue in enumerate((nc.scalar, nc.scalar, nc.sync, nc.sync)):
            queue.dma_start(
                out=x_plane[32 * q : 32 * (q + 1), :T].bitcast(I32),
                in_=x_rows[:, 4 * q : 4 * q + 4, :].broadcast_to([8, 4, T // 4]),
            )
        x_sb = load_words("x_sb", x_words[0])
        w_sb = [load_words("w_first", w_words[0, 0])]
        load_rows(w_plane, w_scales)
        gate_sb = sbuf("gate_sb", [T], F32)
        nc.sync.dma_start(out=gate_sb[:, half(0)], in_=gate[:, half(0)])
        wa_sb = [load_words("wa_first", wa_words[0, 0])]
        adapter_list = load_list("adapter_list", offs2)
        nc.sync.dma_start(out=gate_sb[:, half(1)], in_=gate[:, half(1)])
        w_sb.append(load_words("w_second", w_words[1, 0]))
        load_rows(wa_plane, wa_scales)
        wa_sb.append(load_words("wa_second", wa_words[1, 0]))
        load_rows(wb_plane, wb_scales)
        wb_both = sbuf("wb_sb", [E, N], I32)
        nc.sync.dma_start(out=wb_both[:], in_=wb_words[:, 0].rearrange("e p n d -> p e (n d)").bitcast(I32))
        gate2_sb = sbuf("gate2_sb", [T], F32)
        nc.sync.dma_start(out=gate2_sb[:], in_=gate2)

        def by_place(source):
            return source.rearrange("p (m t) -> p t m", t=PACK)

        wa_placed = [sbuf(f"wa_placed{f}", [PACK, P], U32) for f in range(E)]
        wa_plane_placed = sbuf("wa_plane_placed", [PACK, P], U8)
        nc.gpsimd.tensor_copy(wa_placed[0][:], by_place(wa_sb[0][:].bitcast(U32)))
        nc.gpsimd.tensor_copy(wa_plane_placed[:], by_place(wa_plane[:]))
        nc.gpsimd.tensor_copy(wa_placed[1][:], by_place(wa_sb[1][:].bitcast(U32)))

        def product(acc, weights, weight_plane, words, plane):
            nc.tensor.matmul_mx(
                out=acc,
                lhsT=weights.bitcast(FP8X4),
                lhsT_scale=weight_plane,
                rhs=words.bitcast(FP8X4),
                rhs_scale=plane,
                start=True,
                stop=True,
            )

        def expert_product(acc, j, span):
            e = span.start // C
            product(acc, w_sb[e][:, cols(j * P, P)], w_plane[4 * e :, cols(j * P, P)], xe_words[:, span], xe_plane[:, span])

        def adapter_product(acc, j, f):
            product(acc, wb_both[:, f, cols(j * P, P)], wb_plane[4 * f :, cols(j * P, P)], h_words[f][:], h_planes[f][:])

        def gate_into(by_slot, acc, factor):
            nc.vector.tensor_tensor(by_slot, acc, factor, MULT)

        def twice(factor):
            return factor.unsqueeze(1).broadcast_to([P, 2, C])

        def two_tiles(number, make, tiles, where):
            acc = bank(number, [2, C])
            for place, j in enumerate(tiles):
                make(acc[:, place, :], j, where)
            return acc

        def scatter_on_scalar(by_token, slots, span, by_slot):
            nc.scalar.activation(by_token[:].indirect(entries(slots, span)), by_slot, COPY)

        def scatter_on_vector(by_token, slots, span, by_slot):
            nc.vector.tensor_copy(by_token[:].indirect(entries(slots, span)), by_slot)

        def hidden_block(b):
            f, span = b * P // C, cols(b * P % C, P)
            acc = bank(2 + b, [PACK, P])
            for t in range(PACK):
                product(
                    acc[:, t, :], wa_placed[f][:, t, :], wa_plane_placed[4 * f :, t, :],
                    xa_words[f][:, span], xa_plane[:, cols(b * P, P)],
                )
            nc.scalar.activation(
                grouped[f][:, span, :].rearrange("p (c i) t -> p c t i", i=2),
                acc[:].rearrange("p t (c i) -> p c t i", i=2),
                RELU,
            )

        def gather_adapter_words(name, f):
            words = sbuf(name, [C], U32)
            nc.vector.tensor_copy(words[:], x_sb[:].bitcast(U32).indirect(entries(adapter_list, half(f))))
            xa_words.append(words)

        def quantise(f):
            words, plane = sbuf(f"h_words{f}", [C], U32), sbuf(f"h_plane{f}", [C], U8)
            nc.vector.quantize_mx(
                out=words[:].bitcast(FP8X4), scales=plane[:], in_=grouped[f][:].rearrange("p m d -> p (m d)")
            )
            h_words.append(words)
            h_planes.append(plane)

        def add_and_store(name, j, o_tokens, z_tokens):
            result = sbuf(name, [T], F32)
            nc.gpsimd.tensor_tensor(result[:], o_tokens[:, :T], z_tokens[:, :T], ADD)
            nc.sync.dma_start(out=out[cols(j * P, P), :], in_=result[:])

        everything = cols(0, T)
        blocks = [cols(0, P), cols(P, P)]

        xe_plane, xe_words = sbuf("xe_plane", [T], U8), sbuf("xe_words", [T], U32)
        nc.vector.tensor_copy(xe_plane[:], x_plane[:].indirect(expert_list[:]))
        for span in blocks + [half(1)]:
            nc.vector.tensor_copy(xe_words[:, span], x_sb[:].bitcast(U32).indirect(entries(expert_list, span)))

        y0_tokens, y1_tokens, y2_tokens = (sbuf(f"y_tokens{j}", [T], F32) for j in range(3))

        def first_block(number, b):
            acc = bank(number, [P])
            expert_product(acc[:], 0, blocks[b])
            by_slot = sbuf(f"y0_block{b}", [P], F32)
            gate_into(by_slot[:], acc[:], gate_sb[:, blocks[b]])
            scatter_on_scalar(y0_tokens, expert_list, blocks[b], by_slot[:])

        first_block(0, 0)
        y21 = sbuf("y21_slots", [3, C], F32)
        y1_slots = y21[:, 1:3, :].rearrange("p e c -> p (e c)")
        for number, j, place in ((1, 1, 1), (6, 2, 0)):
            acc = bank(number, [C])
            expert_product(acc[:], j, half(0))
            gate_into(y21[:, place, :], acc[:], gate_sb[:, half(0)])
        early, rest = cols(0, EARLY), cols(EARLY, T - EARLY)
        scatter_on_scalar(y1_tokens, expert_list, early, y1_slots[:, early])
        scatter_on_scalar(y2_tokens, expert_list, half(0), y21[:, 0, :])
        first_block(7, 1)

        xa_plane, xa_words = sbuf("xa_plane", [T], U8), []
        nc.vector.tensor_copy(xa_plane[:], x_plane[:].indirect(adapter_list[:]))
        gather_adapter_words("xa_words0", 0)

        y3_sums = bank(0, [T])
        expert_product(y3_sums[:, half(0)], 3, half(0))
        y1_second_sums = bank(5, [C])
        expert_product(y1_second_sums[:], 1, half(1))
        gate_into(y21[:, 2, :], y1_second_sums[:], gate_sb[:, half(1)])
        expert_product(y3_sums[:, half(1)], 3, half(1))
        y_second_sums = two_tiles(7, expert_product, (0, 2), half(1))

        gather_adapter_words("w_second", 1)
        scatter_on_vector(y1_tokens, expert_list, rest, y1_slots[:, rest])

        grouped = [sbuf(f"grouped{f}", [C, PACK], BF16) for f in range(E)]
        for b in range(T // P):
            hidden_block(b)

        h_words, h_planes = [], []
        y_second = sbuf("wa_placed1", [2, C], F32)
        gate_into(y_second[:], y_second_sums[:], twice(gate_sb[:, half(1)]))
        quantise(0)
        y3_slots = sbuf("w_second", [T], F32)
        gate_into(y3_slots[:], y3_sums[:], gate_sb[:])
        scatter_on_vector(y2_tokens, expert_list, cols(C + P, P), y_second[:, 1, blocks[1]])
        quantise(1)
        scatter_on_scalar(y0_tokens, expert_list, half(1), y_second[:, 0, :])
        scatter_on_scalar(y2_tokens, expert_list, cols(C, P), y_second[:, 1, blocks[0]])

        z12 = sbuf("z12_slots", [2, T], F32)
        z03 = sbuf("z03_slots", [2, T], F32)
        for number, by_slot, tiles, f in (
            (1, z12[:, :, half(0)], (1, 2), 0),
            (6, z03[:, :, half(0)], (0, 3), 0),
            (2, z03[:, :, half(1)], (0, 3), 1),
            (3, z12[:, :, half(1)], (1, 2), 1),
        ):
            gate_into(by_slot, two_tiles(number, adapter_product, tiles, f)[:], twice(gate2_sb[:, half(f)]))

        z1_tokens, z2_tokens = sbuf("z_tokens1", [T], F32), sbuf("z_tokens2", [T], F32)
        for one, two in ((half(0), blocks[0]), (half(1), cols(P, T - P))):
            scatter_on_scalar(z1_tokens, adapter_list, one, z12[:, 0, one])
            scatter_on_scalar(z2_tokens, adapter_list, two, z12[:, 1, two])
        z0_tokens = sbuf("wb_sb", [WIDE], F32)
        scatter_on_vector(z0_tokens, adapter_list, everything, z03[:, 0, :])
        z3_tokens = sbuf("h_words1", [T], F32)
        mine, others = cols(0, LATE), cols(LATE, T - LATE)
        scatter_on_vector(z3_tokens, adapter_list, mine, z03[:, 1, mine])
        scatter_on_scalar(z3_tokens, adapter_list, others, z03[:, 1, others])
        y3_tokens = sbuf("gate2_sb", [WIDE], F32)
        scatter_on_vector(y3_tokens, expert_list, everything, y3_slots[:])

        add_and_store("result1", 1, y1_tokens, z1_tokens)
        add_and_store("z_tokens1", 0, y0_tokens, z0_tokens)
        add_and_store("wb_sb", 2, y2_tokens, z2_tokens)
        final = sbuf("z_tokens2", [T], F32)
        for e in range(2):
            nc.vector.tensor_tensor(final[:, half(e)], y3_tokens[:, half(e)], z3_tokens[:, half(e)], ADD)
            nc.sync.dma_start(out=out[cols(3 * P, P), half(e)], in_=final[:, half(e)])
